import numpy as np
import ml_dtypes


def mxq(x, axis, fmt="e4m3"):
    dtype, down = {"e4m3": (ml_dtypes.float8_e4m3fn, 7), "e5m2": (ml_dtypes.float8_e5m2, 14)}[fmt]
    v = np.moveaxis(np.asarray(x, np.float32).astype(ml_dtypes.bfloat16).astype(np.float64), axis, -1)
    blocks = v.reshape(v.shape[:-1] + (-1, 32))
    amax = np.abs(blocks).max(-1, keepdims=True)
    byte = np.maximum(np.where(amax > 0, np.frexp(amax)[1] - 1 + 127, 0) - down, 1)
    scale = np.exp2(byte - 127.0)
    codes = (blocks / scale).astype(np.float32).astype(dtype).astype(np.float64)
    return np.moveaxis((codes * scale).reshape(v.shape), -1, axis)


WIDE = False


def mx_kscale(k):
    if not WIDE:
        return np.ones(k)
    levels = np.array([10, -10, 5, -5, 0])
    if k % 512:
        return np.exp2(np.random.permutation(np.resize(levels, k // 32))).repeat(32)
    a = np.empty((k // 512, 16))
    for p in range(k // 512):
        a[p, :8] = np.random.permutation(np.resize(levels, 8))
        for g in range(8):
            far = levels[np.abs(levels - a[p, g]) >= 10]
            a[p, g + 8] = far[np.random.randint(len(far))]
    return np.exp2(a.ravel()).repeat(32)


def f64(x):
    return np.asarray(x).astype(np.float64)


def striped(idx):
    return np.tile(idx.reshape(-1, 16).T, (8, 1)).astype(np.uint16)


def unstriped(offs):
    return offs[:16].T.reshape(-1).astype(np.int64)


E2M1 = np.array([0.0, 0.5, 1.0, 1.5, 2.0, 3.0, 4.0, 6.0, -0.0, -0.5, -1.0, -1.5, -2.0, -3.0, -4.0, -6.0])


def pack_weight(w, fmt):
    k, n = w.shape
    w = f64(np.asarray(w, np.float32).astype(ml_dtypes.bfloat16)).reshape(k // 32, 32, n)
    amax = np.abs(w).max(1)
    if fmt == "e4m3":
        byte = np.frexp(amax)[1] - 1 + 127 - 7
    else:
        mant, ex = np.frexp(amax / 6.0)
        byte = np.where(mant > 0.5, ex, ex - 1) + 127
    byte = np.clip(np.where(amax > 0, byte, 1), 1, 254)
    scaled = (w * np.exp2(127.0 - byte)[:, None, :]).reshape(k, n).astype(np.float32)
    by_word = np.ascontiguousarray(scaled.reshape(k // 512, 128, 4, n).transpose(0, 1, 3, 2))
    if fmt == "e4m3":
        words = by_word.astype(ml_dtypes.float8_e4m3fn).view(np.uint8)
    else:
        c = by_word.astype(ml_dtypes.float4_e2m1fn).view(np.uint8) & 0xF
        words = (c[..., 0::2] | (c[..., 1::2] << 4)).reshape(k // 512, 128, 2 * n)
    return np.ascontiguousarray(words), np.ascontiguousarray(byte.astype(np.uint8).reshape(k // 512, 16, n))


def unpack_weight(words, scales, fmt):
    g, _, n = scales.shape
    words = np.ascontiguousarray(words).reshape(g, 128, n, -1)
    if fmt == "e4m3":
        vals = words.view(ml_dtypes.float8_e4m3fn).astype(np.float64)
    else:
        nib = np.empty((g, 128, n, 4), np.uint8)
        nib[..., 0::2] = words & 0xF
        nib[..., 1::2] = words >> 4
        vals = E2M1[nib]
    vals = vals * np.repeat(np.exp2(scales.astype(np.float64) - 127.0), 8, axis=1)[..., None]
    return vals.transpose(0, 1, 3, 2).reshape(g * 512, n)


def gelu(v):
    return 0.5 * v * (1.0 + np.tanh(np.sqrt(2.0 / np.pi) * (v + 0.044715 * v**3)))


K, K2, H, M, N, T, TB, S, P = 1024, 512, 1024, 512, 256, 4096, 2048, 1024, 512

def setup_inputs():
    n = np.random.standard_normal
    s, s2 = mx_kscale(K)[:, None], mx_kscale(K2)[:, None]
    u, um = mx_kscale(H)[:, None], mx_kscale(M)[:, None]
    d = {}
    d["tab_words"], d["tab_scales"] = pack_weight(n((K, T)) * s, "e4m3")
    d["tab2_words"], d["tab2_scales"] = pack_weight(n((K2, TB)) * s2, "e4m3")
    d["offs"] = striped(np.random.permutation(T)[:S])
    d["offs2"] = striped(np.random.permutation(TB)[:P])
    d["pos1"] = striped(np.random.permutation(S)[:P])
    d["w1"] = (1.5 * n((K, H)) / K**0.5 / s * u.T).astype(np.float32)
    d["w2_words"], d["w2_scales"] = pack_weight(1.5 * n((K2, H)) / K2**0.5 / s2, "e2m1")
    d["w3"] = (1.2 * n((K, M)) / K**0.5 / s).astype(np.float32)
    d["lim"] = (np.random.uniform(0.8, 2.2, H) * u[:, 0]).astype(np.float32)
    d["gb"] = (np.random.uniform(0.7, 1.7, H) * u[:, 0]).astype(np.float32)
    d["wgs"] = np.exp(0.3 * n((128, P))).astype(np.float32)
    d["hist"] = n((M, S)).astype(np.float32)
    d["gf"] = (np.random.uniform(0.8, 1.8, M) * um[:, 0]).astype(np.float32)
    d["w4_words"], d["w4_scales"] = pack_weight(n((H, N)) / H**0.5 / u, "e2m1")
    d["w5"] = (n((M, N)) / M**0.5 / um).astype(np.float32)
    return d

def reference(tab_words, tab_scales, tab2_words, tab2_scales, offs, offs2, pos1, w1, w2_words, w2_scales, w3, lim, gb, wgs, hist, gf, w4_words, w4_scales, w5):
    v = unpack_weight(tab_words, tab_scales, "e4m3")[:, unstriped(offs)]
    v2 = unpack_weight(tab2_words, tab2_scales, "e4m3")[:, unstriped(offs2)]
    w2 = unpack_weight(w2_words, w2_scales, "e2m1")
    w4 = unpack_weight(w4_words, w4_scales, "e2m1")
    a = np.abs(mxq(f64(w1), 0, "e4m3").T @ v)
    y2 = w2.T @ v2
    b = f64(gb)[:, None] * (0.5 * y2 * (1.0 + np.tanh(0.7978845608028654 * (y2 + 0.044715 * y2**3))))
    placed = np.zeros((H, S))
    placed[:, unstriped(pos1)] = np.tile(f64(wgs), (H // 128, 1)) * b
    z = np.minimum(a, f64(lim)[:, None]) + placed
    f = f64(gf)[:, None] * np.tanh((mxq(f64(w3), 0, "e4m3").T @ v) + f64(hist))
    return w4.T @ mxq(z, 0, "e4m3") + mxq(f64(w5), 0, "e4m3").T @ mxq(f, 0, "e4m3")

@@ -1,0 +1,298 @@
+from contextlib import ExitStack
+
+import concourse.mybir as mybir
+
+K, K2, H, M, N, T, TB, S, PS = 1024, 512, 1024, 512, 256, 4096, 2048, 1024, 512
+FLOPS = 2 * (K * H * S + K2 * H * PS + K * M * S + H * N * S + M * N * S)
+
+F32 = mybir.dt.float32
+BF16 = mybir.dt.bfloat16
+I32 = mybir.dt.int32
+U32 = mybir.dt.uint32
+U16 = mybir.dt.uint16
+U8 = mybir.dt.uint8
+FP8X4 = mybir.dt.float8_e4m3fn_x4
+FP4X4 = mybir.dt.float4_e2m1fn_x4
+ALU = mybir.AluOpType
+ACT = mybir.ActivationFunctionType
+
+P = 128
+W = 512
+KB = 1024
+
+WGS = 0
+VECS = WGS + 8 * KB
+RAW00 = VECS + 256
+RAW01 = RAW00 + 8 * KB
+RAW11 = RAW01 + 8 * KB
+RAW10 = RAW11 + 8 * KB
+TABS = RAW10 + 8 * KB
+TABW0 = TABS + 4 * KB
+W4 = TABW0 + 16 * KB
+TABW1 = W4 + 1536
+
+
+def tile_list_cylinder_wall_scores_kernel(
+    tc, tab_words, tab_scales, tab2_words, tab2_scales, offs, offs2, pos1, w1, w2_words, w2_scales,
+    w3, lim, gb, wgs, hist, gf, w4_words, w4_scales, w5, out,
+):
+    nc = tc.nc
+    with ExitStack() as ctx:
+        keep = ctx.enter_context(tc.tile_pool(name="keep", bufs=1))
+        shared = ctx.enter_context(tc.tile_pool(name="shared", bufs=1))
+        psum = ctx.enter_context(tc.psum_pool(name="psum", bufs=1))
+
+        def held(name, shape, dtype):
+            return keep.tile(shape, dtype, name=name, align_bytes=64)
+
+        def at(offset, name, shape, dtype):
+            return shared.tile(shape, dtype, name=name, align_bytes=64, offset=offset)
+
+        banks = [psum.tile([P, W], F32, name="bank%d" % i) for i in range(4)]
+        scores = {(n, h): psum.tile([P, W], F32, name="scores%d%d" % (n, h)) for h in range(2) for n in range(2)}
+        staged = [held("staged%d" % i, [P, 4 * W], BF16) for i in range(4)]
+        turn = {"bank": 0, "staged": 0}
+
+        def take(kind, tiles):
+            turn.setdefault(kind, 0)
+            tile = tiles[turn[kind] % len(tiles)]
+            turn[kind] = turn[kind] + 1
+            return tile
+
+        offs_t = keep.tile([P, S // 16], U16, name="offs_t")
+        offs2_t = keep.tile([P, PS // 16], U16, name="offs2_t")
+        pos_t = keep.tile([P, PS // 16], U16, name="pos_t")
+
+        def load_plane(plane, scales, last=nc.sync):
+            rows = 4 * scales.shape[0]
+            for q in range(4):
+                (last if q == 3 else nc.sync).dma_start(plane[32 * q : 32 * q + rows, :].bitcast(I32), scales[:, 4 * q : 4 * q + 4, :].bitcast(I32))
+
+        w2s_raw = at(TABS - 512, "w2s_raw", [P, H], U8)
+        tab2s = at(W4 - 256, "tab2s", [P, TB], U8)
+        w2w_raw = at(VECS - KB, "w2w_raw", [P, 2 * H], U8)
+        tab2w = at(RAW11 - 4 * KB, "tab2w", [P, TB], I32)
+        nc.vector.memset(w2s_raw[:].bitcast(I32), 0)
+        nc.gpsimd.memset(tab2s[:].bitcast(I32), 0)
+        nc.sync.dma_start(offs2_t[:], offs2)
+        nc.sync.dma_start(pos_t[:], pos1)
+        nc.sync.dma_start(offs_t[:], offs)
+        nc.sync.dma_start(w2w_raw[:].bitcast(I32), w2_words[0].bitcast(I32))
+        nc.sync.dma_start(tab2w[:], tab2_words[0].rearrange("p t i -> p (t i)").bitcast(I32))
+        load_plane(w2s_raw, w2_scales)
+        load_plane(tab2s, tab2_scales, nc.gpsimd)
+
+        w2w = held("w2w", [P, 2 * H], U8)
+        w2s = held("w2s", [P, H], U8)
+        v2w = held("v2w", [P, PS], U32)
+        v2s = held("v2s", [P, PS], U8)
+        nc.vector.tensor_copy(
+            w2w[:].bitcast(U16).rearrange("p (b t q) -> p b q t", b=2, t=4),
+            w2w_raw[:].bitcast(U16).rearrange("p (b q t) -> p b q t", b=2, t=4),
+        )
+        nc.vector.tensor_copy(
+            w2s[:].rearrange("p (b t q) -> p b t q", b=2, t=4),
+            w2s_raw[:].rearrange("p (b q t) -> p b t q", b=2, t=4),
+        )
+        nc.vector.tensor_copy(v2w[:], tab2w[:].bitcast(U32).indirect(offs2_t[:]))
+        nc.vector.tensor_copy(v2s[:], tab2s[:].indirect(offs2_t[:]))
+
+        gb_t = at(VECS, "gb_t", [P, 2, 4], F32)
+        lim_t = at(VECS + 64, "lim_t", [P, 2, 4], F32)
+        gf_t = at(VECS + 128, "gf_t", [P, 4], F32)
+        wgs_t = at(WGS, "wgs_t", [P, 4 * PS], F32)
+        nc.sync.dma_start(gb_t[:], gb.rearrange("(b p t) -> p b t", b=2, t=4))
+        for q in (0, 2, 1, 3):
+            nc.sync.dma_start(wgs_t[32 * q : 32 * q + 32, :], wgs.rearrange("(q t) j -> q (t j)", t=4))
+
+        def load_rows(offset, name, rows):
+            raw = at(offset, name, [P, 4, rows.shape[1]], F32)
+            nc.sync.dma_start(raw[:], rows.rearrange("(p j) c -> p j c", j=4))
+            return raw
+
+        w1_raw = {}
+        for a, b, offset in ((0, 0, RAW00), (1, 0, RAW10), (0, 1, RAW01), (1, 1, RAW11)):
+            w1_raw[a, b] = load_rows(offset, "w1_raw%d%d" % (a, b), w1[W * a : W * (a + 1), W * b : W * (b + 1)])
+        nc.sync.dma_start(lim_t[:], lim.rearrange("(b p t) -> p b t", b=2, t=4))
+        nc.sync.dma_start(gf_t[:], gf.rearrange("(p t) -> p t", t=4))
+        tabs = at(TABS, "tabs", [P, T], U8)
+        nc.gpsimd.memset(tabs[:].bitcast(I32), 0)
+        load_plane(tabs, tab_scales)
+        tabw = []
+        for a, offset in ((0, TABW0), (1, TABW1)):
+            words = at(offset, "tabw%d" % a, [P, T], I32)
+            nc.sync.dma_start(words[:], tab_words[a].rearrange("p t i -> p (t i)").bitcast(I32))
+            tabw.append(words)
+
+        gated, pages = {}, {}
+        for u in range(8):
+            b, t = divmod(u, 4)
+            y2 = take("bank", banks)
+            nc.tensor.matmul_mx(
+                y2[:], lhsT=w2w[:, 256 * u : 256 * (u + 1)].bitcast(FP4X4), lhsT_scale=w2s[:, P * u : P * (u + 1)],
+                rhs=v2w[:].bitcast(FP8X4), rhs_scale=v2s[:], start=True, stop=True,
+            )
+            gated[u] = held("g%d" % u, [P, PS], F32)
+            nc.scalar.activation(gated[u][:], y2[:], ACT.Gelu_apprx_tanh)
+            nc.scalar.activation(gated[u][:], gated[u][:], ACT.Copy, scale=gb_t[:, b, t : t + 1])
+
+        def place(u, page, engine):
+            engine.memset(page[:], 0.0)
+            nc.vector.tensor_tensor(page[:].indirect(pos_t[:]), gated[u][:], wgs_t[:, PS * (u % 4) : PS * (u % 4 + 1)], ALU.mult)
+            pages[u] = page
+
+        for u in range(4):
+            place(u, held("page%d" % u, [P, S], F32), nc.gpsimd)
+
+        def quantize(name, grouped, width):
+            codes = held(name + "_codes", [P, width], U32)
+            scales = held(name + "_scales", [P, width], U8)
+            nc.vector.quantize_mx(codes[:].bitcast(FP8X4), scales[:], grouped[:, 0 : 4 * width])
+            return codes, scales
+
+        def quantize_dealt(name, raw):
+            grouped = take("staged", staged)
+            nc.scalar.copy(
+                grouped[:].rearrange("p (t m j) -> p m j t", t=4, j=4),
+                raw[:].rearrange("p j (m t) -> p m j t", t=4),
+            )
+            return quantize(name, grouped, W)
+
+        w1_q = {}
+        for a in range(2):
+            w1_q[a, 0] = quantize_dealt("w1_%d0" % a, w1_raw[a, 0])
+
+        vw, vs = {}, {}
+        for a in range(2):
+            for h in range(2):
+                cols = offs_t[:, 32 * h : 32 * (h + 1)]
+                if a == 0:
+                    vs[h] = held("vs%d" % h, [P, W], U8)
+                    nc.vector.tensor_copy(vs[h][:], tabs[:].indirect(cols))
+                vw[a, h] = held("vw%d%d" % (a, h), [P, W], U32)
+                nc.vector.tensor_copy(vw[a, h][:], tabw[a][:].bitcast(U32).indirect(cols))
+
+        for a in range(2):
+            w1_q[a, 1] = quantize_dealt("w1_%d1" % a, w1_raw[a, 1])
+
+        w5_raw = load_rows(TABS, "w5_raw", w5)
+        w4w = at(W4, "w4w", [P, 2, 2 * N], U8)
+        w4s = at(W4 + KB, "w4s", [P, 2 * N], U8)
+        nc.sync.dma_start(w4w[:].bitcast(I32), w4_words.rearrange("a p c -> p a c").bitcast(I32))
+        nc.gpsimd.memset(w4s[:].bitcast(I32), 0)
+        for q in range(4):
+            nc.sync.dma_start(
+                w4s[32 * q : 32 * q + 4, :].rearrange("r (a n) -> r a n", a=2).bitcast(I32),
+                w4_scales[:, 4 * q : 4 * q + 4, :].rearrange("a r n -> r a n").bitcast(I32),
+            )
+        w3_raw = [load_rows(offset, "w3_raw%d" % a, w3[W * a : W * (a + 1), :]) for a, offset in ((0, RAW00), (1, RAW10))]
+        hist_t = [load_rows(offset, "hist%d" % h, hist[:, W * h : W * (h + 1)]) for h, offset in ((0, RAW01), (1, RAW11))]
+
+        def first_stage(wq, t, h):
+            acc = take("bank", banks)
+            for a in range(2):
+                codes, scales = wq[a]
+                nc.tensor.matmul_mx(
+                    acc[:], lhsT=codes[:, P * t : P * (t + 1)].bitcast(FP8X4), lhsT_scale=scales[:, P * t : P * (t + 1)],
+                    rhs=vw[a, h][:].bitcast(FP8X4), rhs_scale=vs[h][4 * a : P, :], start=(a == 0), stop=(a == 1),
+                )
+            return acc
+
+        def magnitudes(b, h, offsets):
+            mags = []
+            for t in range(4):
+                acc = first_stage([w1_q[0, b], w1_q[1, b]], t, h)
+                mag = at(offsets[t], "mag%d%d%d" % (b, h, t), [P, W], F32)
+                nc.scalar.activation(mag[:], acc[:], ACT.Abs)
+                mags.append(mag)
+            return mags
+
+        def capped(b, h, mags):
+            planes = held("z%d%d" % (b, h), [P, 4, W], BF16)
+            for t in range(4):
+                nc.vector.scalar_tensor_tensor(
+                    planes[:, t, :], mags[t][:], lim_t[:, b, t : t + 1], pages[4 * b + t][:, W * h : W * (h + 1)],
+                    ALU.min, ALU.add,
+                )
+            return planes
+
+        def recalled(h, offsets):
+            pres = []
+            for t in range(4):
+                acc = first_stage(w3_q, t, h)
+                pre = at(offsets[t], "pre%d%d" % (h, t), [P, W], F32)
+                nc.vector.tensor_tensor(pre[:], acc[:], hist_t[h][:, t, :], ALU.add)
+                nc.scalar.activation(pre[:], pre[:], ACT.Tanh)
+                pres.append(pre)
+            return pres
+
+        def gained(h, pres):
+            planes = held("f%d" % h, [P, 4, W], BF16)
+            for t in range(4):
+                nc.vector.tensor_scalar(planes[:, t, :], pres[t][:], gf_t[:, t : t + 1], None, ALU.mult)
+            return planes
+
+        def second_stage(name, planes, h, stationary, start, stop, copy):
+            grouped = take("staged", staged)
+            copy(
+                grouped[:].rearrange("p (c i t) -> p c t i", i=4, t=4),
+                planes[:].rearrange("p t (c i) -> p c t i", i=4),
+            )
+            codes, scales = quantize(name, grouped, W)
+            for n in range(2):
+                lhsT, lhsT_scale = stationary(n)
+                nc.tensor.matmul_mx(
+                    scores[n, h][:], lhsT=lhsT, lhsT_scale=lhsT_scale,
+                    rhs=codes[:].bitcast(FP8X4), rhs_scale=scales[:], start=start, stop=stop,
+                )
+
+        def w4_pass(b):
+            return lambda n: (w4w[:, b, 256 * n : 256 * (n + 1)].bitcast(FP4X4), w4s[:, N * b + P * n : N * b + P * (n + 1)])
+
+        def w5_pass(n):
+            return w5_q[0][:, P * n : P * (n + 1)].bitcast(FP8X4), w5_q[1][:, P * n : P * (n + 1)]
+
+        def store(h):
+            for n in range(2):
+                result = at(RAW10 + 2 * KB * (2 * h + n), "result%d%d" % (n, h), [P, W], F32)
+                if n == 0:
+                    nc.scalar.copy(result[:], scores[n, h][:])
+                else:
+                    nc.vector.tensor_copy(result[:], scores[n, h][:])
+                nc.sync.dma_start(out[P * n : P * (n + 1), W * h : W * (h + 1)], result[:])
+
+        def quarters(*starts):
+            return [s + 2 * KB * i for s in starts for i in range(2)]
+
+        place(4, at(TABW1, "page4", [P, S], F32), nc.gpsimd)
+        mag00 = magnitudes(0, 0, quarters(TABW0, TABW0 + 4 * KB))
+        w3_q = [quantize_dealt("w3_0", w3_raw[0])]
+        z00 = capped(0, 0, mag00)
+        mag01 = magnitudes(0, 1, quarters(TABW0 + 8 * KB, TABW0 + 12 * KB))
+        w3_q.append(quantize_dealt("w3_1", w3_raw[1]))
+        place(5, at(TABW0, "page5", [P, S], F32), nc.gpsimd)
+        z01 = capped(0, 1, mag01)
+        second_stage("zq00", z00, 0, w4_pass(0), True, False, nc.scalar.copy)
+        w5_bf = take("staged", staged)
+        nc.scalar.copy(
+            w5_bf[:, 0 : 4 * N].rearrange("p (c i j) -> p c j i", i=4, j=4),
+            w5_raw[:].rearrange("p j (c i) -> p c j i", i=4),
+        )
+        w5_q = quantize("w5", w5_bf, N)
+        pre0 = recalled(0, quarters(TABW1 + 4 * KB, TABW1 + 8 * KB))
+        place(6, at(TABW0 + 8 * KB, "page6", [P, S], F32), nc.gpsimd)
+        second_stage("zq01", z01, 1, w4_pass(0), True, False, nc.scalar.copy)
+        f0 = gained(0, pre0)
+        mag10 = magnitudes(1, 0, quarters(TABW0 + 4 * KB, TABW0 + 12 * KB))
+        pre1 = recalled(1, quarters(TABW1 + 12 * KB, TABW1 + 8 * KB))
+        place(7, at(TABW1 + 4 * KB, "page7", [P, S], F32), nc.gpsimd)
+        second_stage("fq0", f0, 0, w5_pass, False, False, nc.scalar.copy)
+        mag11 = magnitudes(1, 1, quarters(RAW00, RAW00 + 4 * KB))
+        f1 = gained(1, pre1)
+        z10 = capped(1, 0, mag10)
+        second_stage("fq1", f1, 1, w5_pass, False, False, nc.scalar.copy)
+        z11 = capped(1, 1, mag11)
+        second_stage("zq10", z10, 0, w4_pass(1), False, True, nc.scalar.copy)
+        second_stage("zq11", z11, 1, w4_pass(1), False, True, nc.vector.tensor_copy)
+        store(0)
+        store(1)

@@ -22,14 +22,16 @@ KB = 1024
 
 WGS = 0
 VECS = WGS + 8 * KB
-RAW00 = VECS + 256
-RAW01 = RAW00 + 8 * KB
+RAW00 = VECS + 64
+RAW10 = RAW00 + 8 * KB
+RAW01 = RAW10 + 8 * KB
 RAW11 = RAW01 + 8 * KB
-RAW10 = RAW11 + 8 * KB
-TABS = RAW10 + 8 * KB
-TABW0 = TABS + 4 * KB
-W4 = TABW0 + 16 * KB
-TABW1 = W4 + 1536
+TABW0 = RAW11 + 8 * KB
+TABW1 = TABW0 + 16 * KB
+LATE_VECS = TABW1 + 16 * KB
+RAW30 = LATE_VECS + KB
+RAW31 = RAW30 + 8 * KB
+TABS = RAW31 + 8 * KB
 
 
 def tile_list_cylinder_wall_scores_kernel(
@@ -48,9 +50,8 @@ def tile_list_cylinder_wall_scores_kernel(
         def at(offset, name, shape, dtype):
             return shared.tile(shape, dtype, name=name, align_bytes=64, offset=offset)
 
-        banks = [psum.tile([P, W], F32, name="bank%d" % i) for i in range(4)]
-        scores = {(n, h): psum.tile([P, W], F32, name="scores%d%d" % (n, h)) for h in range(2) for n in range(2)}
-        staged = [held("staged%d" % i, [P, 4 * W], BF16) for i in range(4)]
+        banks = [psum.tile([P, W], F32, name="bank%d" % i) for i in range(8)]
+        staged = [held("staged%d" % i, [P, 4 * W], BF16) for i in range(6)]
         turn = {"bank": 0, "staged": 0}
 
         def take(kind, tiles):
@@ -68,12 +69,12 @@ def tile_list_cylinder_wall_scores_kernel(
             for q in range(4):
                 (last if q == 3 else nc.sync).dma_start(plane[32 * q : 32 * q + rows, :].bitcast(I32), scales[:, 4 * q : 4 * q + 4, :].bitcast(I32))
 
-        w2s_raw = at(TABS - 512, "w2s_raw", [P, H], U8)
-        tab2s = at(W4 - 256, "tab2s", [P, TB], U8)
+        w2s_raw = at(TABW0 - 512, "w2s_raw", [P, H], U8)
+        tab2s = at(LATE_VECS - KB, "tab2s", [P, TB], U8)
         w2w_raw = at(VECS - KB, "w2w_raw", [P, 2 * H], U8)
-        tab2w = at(RAW11 - 4 * KB, "tab2w", [P, TB], I32)
+        tab2w = at(RAW01 - 4 * KB, "tab2w", [P, TB], I32)
         nc.vector.memset(w2s_raw[:].bitcast(I32), 0)
-        nc.gpsimd.memset(tab2s[:].bitcast(I32), 0)
+        nc.vector.memset(tab2s[:].bitcast(I32), 0)
         nc.sync.dma_start(offs2_t[:], offs2)
         nc.sync.dma_start(pos_t[:], pos1)
         nc.sync.dma_start(offs_t[:], offs)
@@ -82,7 +83,16 @@ def tile_list_cylinder_wall_scores_kernel(
         load_plane(w2s_raw, w2_scales)
         load_plane(tab2s, tab2_scales, nc.gpsimd)
 
-        w2w = held("w2w", [P, 2 * H], U8)
+        pages = {}
+
+        def clear(u, page, engine=nc.gpsimd):
+            engine.memset(page[:], 0.0)
+            pages[u] = page
+
+        tabs = at(TABS, "tabs", [P, T], U8)
+        nc.vector.memset(tabs[:].bitcast(I32), 0)
+
+        w2w = at(RAW31 - KB, "w2w", [P, 2 * H], U8)
         w2s = held("w2s", [P, H], U8)
         v2w = held("v2w", [P, PS], U32)
         v2s = held("v2s", [P, PS], U8)
@@ -90,16 +100,16 @@ def tile_list_cylinder_wall_scores_kernel(
             w2w[:].bitcast(U16).rearrange("p (b t q) -> p b q t", b=2, t=4),
             w2w_raw[:].bitcast(U16).rearrange("p (b q t) -> p b q t", b=2, t=4),
         )
+        nc.vector.tensor_copy(v2w[:], tab2w[:].bitcast(U32).indirect(offs2_t[:]))
         nc.vector.tensor_copy(
             w2s[:].rearrange("p (b t q) -> p b t q", b=2, t=4),
             w2s_raw[:].rearrange("p (b q t) -> p b t q", b=2, t=4),
         )
-        nc.vector.tensor_copy(v2w[:], tab2w[:].bitcast(U32).indirect(offs2_t[:]))
         nc.vector.tensor_copy(v2s[:], tab2s[:].indirect(offs2_t[:]))
 
         gb_t = at(VECS, "gb_t", [P, 2, 4], F32)
-        lim_t = at(VECS + 64, "lim_t", [P, 2, 4], F32)
-        gf_t = at(VECS + 128, "gf_t", [P, 4], F32)
+        lim_t = at(LATE_VECS, "lim_t", [P, 2, 4], F32)
+        gf_t = at(LATE_VECS + 64, "gf_t", [P, 4], F32)
         wgs_t = at(WGS, "wgs_t", [P, 4 * PS], F32)
         nc.sync.dma_start(gb_t[:], gb.rearrange("(b p t) -> p b t", b=2, t=4))
         for q in (0, 2, 1, 3):
@@ -111,23 +121,29 @@ def tile_list_cylinder_wall_scores_kernel(
             return raw
 
         w1_raw = {}
-        for a, b, offset in ((0, 0, RAW00), (1, 0, RAW10), (0, 1, RAW01), (1, 1, RAW11)):
-            w1_raw[a, b] = load_rows(offset, "w1_raw%d%d" % (a, b), w1[W * a : W * (a + 1), W * b : W * (b + 1)])
+
+        def load_w1(b, offsets):
+            for a in range(2):
+                w1_raw[a, b] = load_rows(offsets[a], "w1_raw%d%d" % (a, b), w1[W * a : W * (a + 1), W * b : W * (b + 1)])
+
+        load_w1(0, (RAW00, RAW10))
+        load_w1(1, (RAW01, RAW11))
         nc.sync.dma_start(lim_t[:], lim.rearrange("(b p t) -> p b t", b=2, t=4))
         nc.sync.dma_start(gf_t[:], gf.rearrange("(p t) -> p t", t=4))
-        tabs = at(TABS, "tabs", [P, T], U8)
-        nc.gpsimd.memset(tabs[:].bitcast(I32), 0)
         load_plane(tabs, tab_scales)
-        tabw = []
-        for a, offset in ((0, TABW0), (1, TABW1)):
+
+        def load_words(a, offset):
             words = at(offset, "tabw%d" % a, [P, T], I32)
             nc.sync.dma_start(words[:], tab_words[a].rearrange("p t i -> p (t i)").bitcast(I32))
-            tabw.append(words)
+            return words
 
-        gated, pages = {}, {}
+        tabw = [load_words(0, TABW0)]
+        tabw.append(load_words(1, TABW1))
+
+        gated = {}
         for u in range(8):
             b, t = divmod(u, 4)
-            y2 = take("bank", banks)
+            y2 = banks[0] if u == 1 else take("bank", banks)
             nc.tensor.matmul_mx(
                 y2[:], lhsT=w2w[:, 256 * u : 256 * (u + 1)].bitcast(FP4X4), lhsT_scale=w2s[:, P * u : P * (u + 1)],
                 rhs=v2w[:].bitcast(FP8X4), rhs_scale=v2s[:], start=True, stop=True,
@@ -136,48 +152,52 @@ def tile_list_cylinder_wall_scores_kernel(
             nc.scalar.activation(gated[u][:], y2[:], ACT.Gelu_apprx_tanh)
             nc.scalar.activation(gated[u][:], gated[u][:], ACT.Copy, scale=gb_t[:, b, t : t + 1])
 
-        def place(u, page, engine):
-            engine.memset(page[:], 0.0)
-            nc.vector.tensor_tensor(page[:].indirect(pos_t[:]), gated[u][:], wgs_t[:, PS * (u % 4) : PS * (u % 4 + 1)], ALU.mult)
-            pages[u] = page
+        w3_raw = [load_rows(offset, "w3_raw%d" % a, w3[W * a : W * (a + 1), :]) for a, offset in ((0, RAW30), (1, RAW31))]
+
+        def place(u):
+            nc.vector.tensor_tensor(pages[u][:].indirect(pos_t[:]), gated[u][:], wgs_t[:, PS * (u % 4) : PS * (u % 4 + 1)], ALU.mult)
 
         for u in range(4):
-            place(u, held("page%d" % u, [P, S], F32), nc.gpsimd)
+            clear(u, held("page%d" % u, [P, S], F32), nc.vector)
+            place(u)
 
-        def quantize(name, grouped, width):
-            codes = held(name + "_codes", [P, width], U32)
-            scales = held(name + "_scales", [P, width], U8)
+        def quantize(name, grouped, width, offset=None):
+            if offset is None:
+                codes = held(name + "_codes", [P, width], U32)
+                scales = held(name + "_scales", [P, width], U8)
+            else:
+                codes = at(offset, name + "_codes", [P, width], U32)
+                scales = at(offset + 4 * width, name + "_scales", [P, width], U8)
             nc.vector.quantize_mx(codes[:].bitcast(FP8X4), scales[:], grouped[:, 0 : 4 * width])
             return codes, scales
 
-        def quantize_dealt(name, raw):
+        def quantize_dealt(name, raw, offset=None):
             grouped = take("staged", staged)
             nc.scalar.copy(
                 grouped[:].rearrange("p (t m j) -> p m j t", t=4, j=4),
                 raw[:].rearrange("p j (m t) -> p m j t", t=4),
             )
-            return quantize(name, grouped, W)
+            return quantize(name, grouped, W, offset)
 
         w1_q = {}
         for a in range(2):
             w1_q[a, 0] = quantize_dealt("w1_%d0" % a, w1_raw[a, 0])
 
         vw, vs = {}, {}
-        for a in range(2):
-            for h in range(2):
-                cols = offs_t[:, 32 * h : 32 * (h + 1)]
-                if a == 0:
-                    vs[h] = held("vs%d" % h, [P, W], U8)
-                    nc.vector.tensor_copy(vs[h][:], tabs[:].indirect(cols))
+        for h in range(2):
+            cols = offs_t[:, 32 * h : 32 * (h + 1)]
+            vs[h] = held("vs%d" % h, [P, W], U8)
+            nc.vector.tensor_copy(vs[h][:], tabs[:].indirect(cols))
+            for a in range(2):
                 vw[a, h] = held("vw%d%d" % (a, h), [P, W], U32)
                 nc.vector.tensor_copy(vw[a, h][:], tabw[a][:].bitcast(U32).indirect(cols))
 
         for a in range(2):
-            w1_q[a, 1] = quantize_dealt("w1_%d1" % a, w1_raw[a, 1])
+            w1_q[a, 1] = quantize_dealt("w1_%d1" % a, w1_raw[a, 1], TABW1 + 4 * KB + 2560 * a)
 
-        w5_raw = load_rows(TABS, "w5_raw", w5)
-        w4w = at(W4, "w4w", [P, 2, 2 * N], U8)
-        w4s = at(W4 + KB, "w4s", [P, 2 * N], U8)
+        w5_raw = load_rows(RAW01, "w5_raw", w5)
+        w4w = at(RAW01 + 4 * KB, "w4w", [P, 2, 2 * N], U8)
+        w4s = at(RAW01 + 5 * KB, "w4s", [P, 2 * N], U8)
         nc.sync.dma_start(w4w[:].bitcast(I32), w4_words.rearrange("a p c -> p a c").bitcast(I32))
         nc.gpsimd.memset(w4s[:].bitcast(I32), 0)
         for q in range(4):
@@ -185,8 +205,7 @@ def tile_list_cylinder_wall_scores_kernel(
                 w4s[32 * q : 32 * q + 4, :].rearrange("r (a n) -> r a n", a=2).bitcast(I32),
                 w4_scales[:, 4 * q : 4 * q + 4, :].rearrange("a r n -> r a n").bitcast(I32),
             )
-        w3_raw = [load_rows(offset, "w3_raw%d" % a, w3[W * a : W * (a + 1), :]) for a, offset in ((0, RAW00), (1, RAW10))]
-        hist_t = [load_rows(offset, "hist%d" % h, hist[:, W * h : W * (h + 1)]) for h, offset in ((0, RAW01), (1, RAW11))]
+        hist_t = [load_rows(offset, "hist%d" % h, hist[:, W * h : W * (h + 1)]) for h, offset in ((0, RAW00), (1, RAW10))]
 
         def first_stage(wq, t, h):
             acc = take("bank", banks)
@@ -222,28 +241,36 @@ def tile_list_cylinder_wall_scores_kernel(
                 acc = first_stage(w3_q, t, h)
                 pre = at(offsets[t], "pre%d%d" % (h, t), [P, W], F32)
                 nc.vector.tensor_tensor(pre[:], acc[:], hist_t[h][:, t, :], ALU.add)
-                nc.scalar.activation(pre[:], pre[:], ACT.Tanh)
                 pres.append(pre)
             return pres
 
-        def gained(h, pres):
+        def gained(h, pres, on_vector=0):
             planes = held("f%d" % h, [P, 4, W], BF16)
             for t in range(4):
+                nc.scalar.activation(pres[t][:], pres[t][:], ACT.Tanh)
+            for t in range(on_vector):
                 nc.vector.tensor_scalar(planes[:, t, :], pres[t][:], gf_t[:, t : t + 1], None, ALU.mult)
+            for t in range(on_vector, 4):
+                nc.scalar.activation(planes[:, t, :], pres[t][:], ACT.Copy, scale=gf_t[:, t : t + 1])
             return planes
 
-        def second_stage(name, planes, h, stationary, start, stop, copy):
+        def woven(name, planes, shares=((0, W, nc.scalar.copy),)):
             grouped = take("staged", staged)
-            copy(
-                grouped[:].rearrange("p (c i t) -> p c t i", i=4, t=4),
-                planes[:].rearrange("p t (c i) -> p c t i", i=4),
-            )
-            codes, scales = quantize(name, grouped, W)
-            for n in range(2):
-                lhsT, lhsT_scale = stationary(n)
+            for c0, c1, copy in shares:
+                copy(
+                    grouped[:, 4 * c0 : 4 * c1].rearrange("p (c i t) -> p c t i", i=4, t=4),
+                    planes[:, :, c0:c1].rearrange("p t (c i) -> p c t i", i=4),
+                )
+            return quantize(name, grouped, W)
+
+        def second_stage(acc, n, stationary, moving, start, stop, c0=0, width=W, step=W):
+            lhsT, lhsT_scale = stationary(n)
+            codes, scales = moving
+            for c in range(0, width, step):
                 nc.tensor.matmul_mx(
-                    scores[n, h][:], lhsT=lhsT, lhsT_scale=lhsT_scale,
-                    rhs=codes[:].bitcast(FP8X4), rhs_scale=scales[:], start=start, stop=stop,
+                    acc[:, c0 + c : c0 + c + step], lhsT=lhsT, lhsT_scale=lhsT_scale,
+                    rhs=codes[:, c : c + step].bitcast(FP8X4), rhs_scale=scales[:, c : c + step],
+                    start=start, stop=stop and c + step == width,
                 )
 
         def w4_pass(b):
@@ -252,47 +279,61 @@ def tile_list_cylinder_wall_scores_kernel(
         def w5_pass(n):
             return w5_q[0][:, P * n : P * (n + 1)].bitcast(FP8X4), w5_q[1][:, P * n : P * (n + 1)]
 
-        def store(h):
+        def store(scores, h, c0, width):
             for n in range(2):
-                result = at(RAW10 + 2 * KB * (2 * h + n), "result%d%d" % (n, h), [P, W], F32)
+                result = at(RAW30 + 2 * KB * (2 * h + n) + 4 * c0, "result%d%d_%d" % (n, h, c0), [P, width], F32)
                 if n == 0:
-                    nc.scalar.copy(result[:], scores[n, h][:])
+                    nc.scalar.copy(result[:], scores[n][:, c0 : c0 + width])
                 else:
-                    nc.vector.tensor_copy(result[:], scores[n, h][:])
-                nc.sync.dma_start(out[P * n : P * (n + 1), W * h : W * (h + 1)], result[:])
+                    nc.vector.tensor_copy(result[:], scores[n][:, c0 : c0 + width])
+                nc.sync.dma_start(out[P * n : P * (n + 1), W * h + c0 : W * h + c0 + width], result[:])
 
         def quarters(*starts):
             return [s + 2 * KB * i for s in starts for i in range(2)]
 
-        place(4, at(TABW1, "page4", [P, S], F32), nc.gpsimd)
+        def quantize_w5():
+            grouped = take("staged", staged)
+            nc.scalar.copy(
+                grouped[:, 0 : 4 * N].rearrange("p (c i j) -> p c j i", i=4, j=4),
+                w5_raw[:].rearrange("p j (c i) -> p c j i", i=4),
+            )
+            return quantize("w5", grouped, N)
+
         mag00 = magnitudes(0, 0, quarters(TABW0, TABW0 + 4 * KB))
-        w3_q = [quantize_dealt("w3_0", w3_raw[0])]
-        z00 = capped(0, 0, mag00)
+        w3_q = [quantize_dealt("w3_%d" % a, w3_raw[a]) for a in range(2)]
         mag01 = magnitudes(0, 1, quarters(TABW0 + 8 * KB, TABW0 + 12 * KB))
-        w3_q.append(quantize_dealt("w3_1", w3_raw[1]))
-        place(5, at(TABW0, "page5", [P, S], F32), nc.gpsimd)
+        clear(4, at(TABW1, "page4", [P, S], F32), nc.vector)
+        place(4)
+        z00 = capped(0, 0, mag00)
+        pre0 = recalled(0, quarters(RAW30, RAW30 + 4 * KB))
+        w5_q = quantize_w5()
+        zq00 = woven("zq00", z00)
         z01 = capped(0, 1, mag01)
-        second_stage("zq00", z00, 0, w4_pass(0), True, False, nc.scalar.copy)
-        w5_bf = take("staged", staged)
-        nc.scalar.copy(
-            w5_bf[:, 0 : 4 * N].rearrange("p (c i j) -> p c j i", i=4, j=4),
-            w5_raw[:].rearrange("p j (c i) -> p c j i", i=4),
-        )
-        w5_q = quantize("w5", w5_bf, N)
-        pre0 = recalled(0, quarters(TABW1 + 4 * KB, TABW1 + 8 * KB))
-        place(6, at(TABW0 + 8 * KB, "page6", [P, S], F32), nc.gpsimd)
-        second_stage("zq01", z01, 1, w4_pass(0), True, False, nc.scalar.copy)
+        clear(5, at(RAW00, "page5", [P, S], F32))
+        place(5)
         f0 = gained(0, pre0)
-        mag10 = magnitudes(1, 0, quarters(TABW0 + 4 * KB, TABW0 + 12 * KB))
-        pre1 = recalled(1, quarters(TABW1 + 12 * KB, TABW1 + 8 * KB))
-        place(7, at(TABW1 + 4 * KB, "page7", [P, S], F32), nc.gpsimd)
-        second_stage("fq0", f0, 0, w5_pass, False, False, nc.scalar.copy)
-        mag11 = magnitudes(1, 1, quarters(RAW00, RAW00 + 4 * KB))
-        f1 = gained(1, pre1)
+        pre1 = recalled(1, quarters(RAW31, RAW31 + 4 * KB))
+        fq0 = woven("fq0", f0)
+        mag10 = magnitudes(1, 0, quarters(RAW11, RAW11 + 4 * KB))
+        clear(6, at(TABW0 + 12 * KB, "page6", [P, S], F32))
+        place(6)
+        clear(7, at(RAW10, "page7", [P, S], F32))
+        place(7)
+        f1 = gained(1, pre1, 0)
+        zq01 = woven("zq01", z01)
+        fq1 = woven("fq1", f1)
+        mag11 = magnitudes(1, 1, quarters(TABW0, TABW0 + 4 * KB))
         z10 = capped(1, 0, mag10)
-        second_stage("fq1", f1, 1, w5_pass, False, False, nc.scalar.copy)
         z11 = capped(1, 1, mag11)
-        second_stage("zq10", z10, 0, w4_pass(1), False, True, nc.scalar.copy)
-        second_stage("zq11", z11, 1, w4_pass(1), False, True, nc.vector.tensor_copy)
-        store(0)
-        store(1)
+        zq10 = woven("zq10", z10)
+
+        def finish(h, parts):
+            scores = [take("bank", banks) for n in range(2)]
+            for i, stationary in enumerate((w4_pass(0), w5_pass, w4_pass(1))):
+                for n in range(2):
+                    second_stage(scores[n], n, stationary, parts[i], i == 0, i == 2)
+            store(scores, h, 0, W)
+
+        finish(0, (zq00, fq0, zq10))
+        zq11 = woven("zq11", z11, ((0, 192, nc.scalar.copy), (192, W, nc.vector.tensor_copy)))
+        finish(1, (zq01, fq1, zq11))

@@ -23,13 +23,13 @@ KB = 1024
 WGS = 0
 VECS = WGS + 8 * KB
 RAW00 = VECS + 64
-RAW10 = RAW00 + 8 * KB
-RAW01 = RAW10 + 8 * KB
-RAW11 = RAW01 + 8 * KB
+RAW01 = RAW00 + 8 * KB
+RAW10 = RAW01 + 8 * KB
+RAW11 = RAW10 + 8 * KB
 TABW0 = RAW11 + 8 * KB
 TABW1 = TABW0 + 16 * KB
 LATE_VECS = TABW1 + 16 * KB
-RAW30 = LATE_VECS + KB
+RAW30 = LATE_VECS + 1536
 RAW31 = RAW30 + 8 * KB
 TABS = RAW31 + 8 * KB
 
@@ -64,24 +64,26 @@ def tile_list_cylinder_wall_scores_kernel(
         offs2_t = keep.tile([P, PS // 16], U16, name="offs2_t")
         pos_t = keep.tile([P, PS // 16], U16, name="pos_t")
 
-        def load_plane(plane, scales, last=nc.sync):
+        def load_plane(plane, scales, queues):
             rows = 4 * scales.shape[0]
             for q in range(4):
-                (last if q == 3 else nc.sync).dma_start(plane[32 * q : 32 * q + rows, :].bitcast(I32), scales[:, 4 * q : 4 * q + 4, :].bitcast(I32))
+                queues[q].dma_start(plane[32 * q : 32 * q + rows, :].bitcast(I32), scales[:, 4 * q : 4 * q + 4, :].bitcast(I32))
 
-        w2s_raw = at(TABW0 - 512, "w2s_raw", [P, H], U8)
-        tab2s = at(LATE_VECS - KB, "tab2s", [P, TB], U8)
-        w2w_raw = at(VECS - KB, "w2w_raw", [P, 2 * H], U8)
-        tab2w = at(RAW01 - 4 * KB, "tab2w", [P, TB], I32)
+        w2s_raw = at(TABW0, "w2s_raw", [P, H], U8)
+        tab2s = at(LATE_VECS - 512, "tab2s", [P, TB], U8)
+        w2w_raw = at(RAW00 - 2 * KB, "w2w_raw", [P, 2 * H], U8)
+        tab2w = at(RAW10 - 4 * KB, "tab2w", [P, TB], I32)
         nc.vector.memset(w2s_raw[:].bitcast(I32), 0)
         nc.vector.memset(tab2s[:].bitcast(I32), 0)
+        gb_t = held("gb_t", [P, 2, 4], F32)
+        nc.gpsimd.dma_start(gb_t[:], gb.rearrange("(b p t) -> p b t", b=2, t=4))
         nc.sync.dma_start(offs2_t[:], offs2)
         nc.sync.dma_start(pos_t[:], pos1)
         nc.sync.dma_start(offs_t[:], offs)
         nc.sync.dma_start(w2w_raw[:].bitcast(I32), w2_words[0].bitcast(I32))
         nc.sync.dma_start(tab2w[:], tab2_words[0].rearrange("p t i -> p (t i)").bitcast(I32))
-        load_plane(w2s_raw, w2_scales)
-        load_plane(tab2s, tab2_scales, nc.gpsimd)
+        load_plane(w2s_raw, w2_scales, [nc.sync] * 4)
+        load_plane(tab2s, tab2_scales, [nc.sync] * 3 + [nc.gpsimd])
 
         pages = {}
 
@@ -107,30 +109,21 @@ def tile_list_cylinder_wall_scores_kernel(
         )
         nc.vector.tensor_copy(v2s[:], tab2s[:].indirect(offs2_t[:]))
 
-        gb_t = at(VECS, "gb_t", [P, 2, 4], F32)
         lim_t = at(LATE_VECS, "lim_t", [P, 2, 4], F32)
         gf_t = at(LATE_VECS + 64, "gf_t", [P, 4], F32)
         wgs_t = at(WGS, "wgs_t", [P, 4 * PS], F32)
-        nc.sync.dma_start(gb_t[:], gb.rearrange("(b p t) -> p b t", b=2, t=4))
+        load_plane(tabs, tab_scales, [nc.sync] * 4)
         for q in (0, 2, 1, 3):
-            nc.sync.dma_start(wgs_t[32 * q : 32 * q + 32, :], wgs.rearrange("(q t) j -> q (t j)", t=4))
+            (nc.sync if q < 2 else nc.scalar).dma_start(wgs_t[32 * q : 32 * q + 32, :], wgs.rearrange("(q t) j -> q (t j)", t=4))
 
         def load_rows(offset, name, rows):
             raw = at(offset, name, [P, 4, rows.shape[1]], F32)
             nc.sync.dma_start(raw[:], rows.rearrange("(p j) c -> p j c", j=4))
             return raw
 
-        w1_raw = {}
-
-        def load_w1(b, offsets):
-            for a in range(2):
-                w1_raw[a, b] = load_rows(offsets[a], "w1_raw%d%d" % (a, b), w1[W * a : W * (a + 1), W * b : W * (b + 1)])
-
-        load_w1(0, (RAW00, RAW10))
-        load_w1(1, (RAW01, RAW11))
+        w1_raw = [load_rows(offset, "w1_raw%d" % a, w1[W * a : W * (a + 1), :]) for a, offset in ((0, RAW00), (1, RAW10))]
         nc.sync.dma_start(lim_t[:], lim.rearrange("(b p t) -> p b t", b=2, t=4))
         nc.sync.dma_start(gf_t[:], gf.rearrange("(p t) -> p t", t=4))
-        load_plane(tabs, tab_scales)
 
         def load_words(a, offset):
             words = at(offset, "tabw%d" % a, [P, T], I32)
@@ -140,10 +133,15 @@ def tile_list_cylinder_wall_scores_kernel(
         tabw = [load_words(0, TABW0)]
         tabw.append(load_words(1, TABW1))
 
+        vs = {}
+        for h in range(2):
+            vs[h] = at(LATE_VECS + 128 + W * h, "vs%d" % h, [P, W], U8)
+            nc.vector.tensor_copy(vs[h][:], tabs[:].indirect(offs_t[:, 32 * h : 32 * (h + 1)]))
+
         gated = {}
         for u in range(8):
             b, t = divmod(u, 4)
-            y2 = banks[0] if u == 1 else take("bank", banks)
+            y2 = take("bank", banks)
             nc.tensor.matmul_mx(
                 y2[:], lhsT=w2w[:, 256 * u : 256 * (u + 1)].bitcast(FP4X4), lhsT_scale=w2s[:, P * u : P * (u + 1)],
                 rhs=v2w[:].bitcast(FP8X4), rhs_scale=v2s[:], start=True, stop=True,
@@ -175,26 +173,25 @@ def tile_list_cylinder_wall_scores_kernel(
             grouped = take("staged", staged)
             nc.scalar.copy(
                 grouped[:].rearrange("p (t m j) -> p m j t", t=4, j=4),
-                raw[:].rearrange("p j (m t) -> p m j t", t=4),
+                raw.rearrange("p j (m t) -> p m j t", t=4),
             )
             return quantize(name, grouped, W, offset)
 
         w1_q = {}
         for a in range(2):
-            w1_q[a, 0] = quantize_dealt("w1_%d0" % a, w1_raw[a, 0])
+            w1_q[a, 0] = quantize_dealt("w1_%d0" % a, w1_raw[a][:, :, 0:W])
 
-        vw, vs = {}, {}
+        vw = {}
         for h in range(2):
             cols = offs_t[:, 32 * h : 32 * (h + 1)]
-            vs[h] = held("vs%d" % h, [P, W], U8)
-            nc.vector.tensor_copy(vs[h][:], tabs[:].indirect(cols))
             for a in range(2):
                 vw[a, h] = held("vw%d%d" % (a, h), [P, W], U32)
                 nc.vector.tensor_copy(vw[a, h][:], tabw[a][:].bitcast(U32).indirect(cols))
 
         for a in range(2):
-            w1_q[a, 1] = quantize_dealt("w1_%d1" % a, w1_raw[a, 1], TABW1 + 4 * KB + 2560 * a)
+            w1_q[a, 1] = quantize_dealt("w1_%d1" % a, w1_raw[a][:, :, W : 2 * W], TABW1 + 4 * KB + 2560 * a)
 
+        hist_t = [load_rows(offset, "hist%d" % h, hist[:, W * h : W * (h + 1)]) for h, offset in ((0, RAW00), (1, RAW10))]
         w5_raw = load_rows(RAW01, "w5_raw", w5)
         w4w = at(RAW01 + 4 * KB, "w4w", [P, 2, 2 * N], U8)
         w4s = at(RAW01 + 5 * KB, "w4s", [P, 2 * N], U8)
@@ -205,7 +202,6 @@ def tile_list_cylinder_wall_scores_kernel(
                 w4s[32 * q : 32 * q + 4, :].rearrange("r (a n) -> r a n", a=2).bitcast(I32),
                 w4_scales[:, 4 * q : 4 * q + 4, :].rearrange("a r n -> r a n").bitcast(I32),
             )
-        hist_t = [load_rows(offset, "hist%d" % h, hist[:, W * h : W * (h + 1)]) for h, offset in ((0, RAW00), (1, RAW10))]
 
         def first_stage(wq, t, h):
             acc = take("bank", banks)
@@ -282,7 +278,7 @@ def tile_list_cylinder_wall_scores_kernel(
         def store(scores, h, c0, width):
             for n in range(2):
                 result = at(RAW30 + 2 * KB * (2 * h + n) + 4 * c0, "result%d%d_%d" % (n, h, c0), [P, width], F32)
-                if n == 0:
+                if n == 0 or h == 0:
                     nc.scalar.copy(result[:], scores[n][:, c0 : c0 + width])
                 else:
                     nc.vector.tensor_copy(result[:], scores[n][:, c0 : c0 + width])
@@ -293,14 +289,14 @@ def tile_list_cylinder_wall_scores_kernel(
 
         def quantize_w5():
             grouped = take("staged", staged)
-            nc.scalar.copy(
+            nc.vector.tensor_copy(
                 grouped[:, 0 : 4 * N].rearrange("p (c i j) -> p c j i", i=4, j=4),
                 w5_raw[:].rearrange("p j (c i) -> p c j i", i=4),
             )
             return quantize("w5", grouped, N)
 
         mag00 = magnitudes(0, 0, quarters(TABW0, TABW0 + 4 * KB))
-        w3_q = [quantize_dealt("w3_%d" % a, w3_raw[a]) for a in range(2)]
+        w3_q = [quantize_dealt("w3_%d" % a, w3_raw[a][:]) for a in range(2)]
         mag01 = magnitudes(0, 1, quarters(TABW0 + 8 * KB, TABW0 + 12 * KB))
         clear(4, at(TABW1, "page4", [P, S], F32), nc.vector)
         place(4)
@@ -321,7 +317,6 @@ def tile_list_cylinder_wall_scores_kernel(
         place(7)
         f1 = gained(1, pre1, 0)
         zq01 = woven("zq01", z01)
-        fq1 = woven("fq1", f1)
         mag11 = magnitudes(1, 1, quarters(TABW0, TABW0 + 4 * KB))
         z10 = capped(1, 0, mag10)
         z11 = capped(1, 1, mag11)
@@ -329,11 +324,12 @@ def tile_list_cylinder_wall_scores_kernel(
 
         def finish(h, parts):
             scores = [take("bank", banks) for n in range(2)]
-            for i, stationary in enumerate((w4_pass(0), w5_pass, w4_pass(1))):
+            for i, (stationary, moving) in enumerate(parts):
                 for n in range(2):
-                    second_stage(scores[n], n, stationary, parts[i], i == 0, i == 2)
+                    second_stage(scores[n], n, stationary, moving, i == 0, i == 2)
             store(scores, h, 0, W)
 
-        finish(0, (zq00, fq0, zq10))
-        zq11 = woven("zq11", z11, ((0, 192, nc.scalar.copy), (192, W, nc.vector.tensor_copy)))
-        finish(1, (zq01, fq1, zq11))
+        finish(0, ((w4_pass(0), zq00), (w5_pass, fq0), (w4_pass(1), zq10)))
+        fq1 = woven("fq1", f1)
+        zq11 = woven("zq11", z11, ((0, W, nc.vector.tensor_copy),))
+        finish(1, ((w4_pass(0), zq01), (w4_pass(1), zq11), (w5_pass, fq1)))

@@ -1,6 +1,7 @@
 from contextlib import ExitStack
 
 import concourse.mybir as mybir
+from concourse.masks import make_identity
 
 K, K2, H, M, N, T, TB, S, PS = 1024, 512, 1024, 512, 256, 4096, 2048, 1024, 512
 FLOPS = 2 * (K * H * S + K2 * H * PS + K * M * S + H * N * S + M * N * S)
@@ -19,19 +20,20 @@ ACT = mybir.ActivationFunctionType
 P = 128
 W = 512
 KB = 1024
+STAGING_TILES = 6
 
 WGS = 0
-VECS = WGS + 8 * KB
-RAW00 = VECS + 64
-RAW01 = RAW00 + 8 * KB
-RAW10 = RAW01 + 8 * KB
-RAW11 = RAW10 + 8 * KB
-TABW0 = RAW11 + 8 * KB
-TABW1 = TABW0 + 16 * KB
-LATE_VECS = TABW1 + 16 * KB
-RAW30 = LATE_VECS + 1536
-RAW31 = RAW30 + 8 * KB
-TABS = RAW31 + 8 * KB
+GB = WGS + 8 * KB
+W1_A0 = GB + 64
+W1_A1 = W1_A0 + 16 * KB
+TAB_A0 = W1_A1 + 16 * KB
+TAB_A1 = TAB_A0 + 16 * KB
+SMALL = TAB_A1 + 16 * KB
+W3_A0 = SMALL + 1536
+W3_A1 = W3_A0 + 8 * KB
+STAGING = W3_A1 + 8 * KB
+W5 = STAGING + 4 * KB * STAGING_TILES
+TAB_PLANE = W5 + 4 * KB
 
 
 def tile_list_cylinder_wall_scores_kernel(
@@ -51,113 +53,138 @@ def tile_list_cylinder_wall_scores_kernel(
             return shared.tile(shape, dtype, name=name, align_bytes=64, offset=offset)
 
         banks = [psum.tile([P, W], F32, name="bank%d" % i) for i in range(8)]
-        staged = [held("staged%d" % i, [P, 4 * W], BF16) for i in range(6)]
-        turn = {"bank": 0, "staged": 0}
+        staging = [at(STAGING + 4 * KB * i, "staging%d" % i, [P, 4 * W], BF16) for i in range(STAGING_TILES)]
+        rings = {"scan": banks, "w1": banks[0:4], "w3": banks[4:8], "staging": staging}
+        turns = {ring: 0 for ring in rings}
 
-        def take(kind, tiles):
-            turn.setdefault(kind, 0)
-            tile = tiles[turn[kind] % len(tiles)]
-            turn[kind] = turn[kind] + 1
+        def take(ring):
+            tile = rings[ring][turns[ring] % len(rings[ring])]
+            turns[ring] = turns[ring] + 1
             return tile
-
-        offs_t = keep.tile([P, S // 16], U16, name="offs_t")
-        offs2_t = keep.tile([P, PS // 16], U16, name="offs2_t")
-        pos_t = keep.tile([P, PS // 16], U16, name="pos_t")
 
         def load_plane(plane, scales, queues):
             rows = 4 * scales.shape[0]
             for q in range(4):
                 queues[q].dma_start(plane[32 * q : 32 * q + rows, :].bitcast(I32), scales[:, 4 * q : 4 * q + 4, :].bitcast(I32))
 
-        w2s_raw = at(TABW0, "w2s_raw", [P, H], U8)
-        tab2s = at(LATE_VECS - 512, "tab2s", [P, TB], U8)
-        w2w_raw = at(RAW00 - 2 * KB, "w2w_raw", [P, 2 * H], U8)
-        tab2w = at(RAW10 - 4 * KB, "tab2w", [P, TB], I32)
-        nc.vector.memset(w2s_raw[:].bitcast(I32), 0)
-        nc.vector.memset(tab2s[:].bitcast(I32), 0)
-        gb_t = held("gb_t", [P, 2, 4], F32)
-        nc.gpsimd.dma_start(gb_t[:], gb.rearrange("(b p t) -> p b t", b=2, t=4))
-        nc.sync.dma_start(offs2_t[:], offs2)
-        nc.sync.dma_start(pos_t[:], pos1)
-        nc.sync.dma_start(offs_t[:], offs)
-        nc.sync.dma_start(w2w_raw[:].bitcast(I32), w2_words[0].bitcast(I32))
-        nc.sync.dma_start(tab2w[:], tab2_words[0].rearrange("p t i -> p (t i)").bitcast(I32))
-        load_plane(w2s_raw, w2_scales, [nc.sync] * 4)
-        load_plane(tab2s, tab2_scales, [nc.sync] * 3 + [nc.gpsimd])
-
-        pages = {}
-
-        def clear(u, page, engine=nc.gpsimd):
-            engine.memset(page[:], 0.0)
-            pages[u] = page
-
-        tabs = at(TABS, "tabs", [P, T], U8)
-        nc.vector.memset(tabs[:].bitcast(I32), 0)
-
-        w2w = at(RAW31 - KB, "w2w", [P, 2 * H], U8)
-        w2s = held("w2s", [P, H], U8)
-        v2w = held("v2w", [P, PS], U32)
-        v2s = held("v2s", [P, PS], U8)
-        nc.vector.tensor_copy(
-            w2w[:].bitcast(U16).rearrange("p (b t q) -> p b q t", b=2, t=4),
-            w2w_raw[:].bitcast(U16).rearrange("p (b q t) -> p b q t", b=2, t=4),
-        )
-        nc.vector.tensor_copy(v2w[:], tab2w[:].bitcast(U32).indirect(offs2_t[:]))
-        nc.vector.tensor_copy(
-            w2s[:].rearrange("p (b t q) -> p b t q", b=2, t=4),
-            w2s_raw[:].rearrange("p (b q t) -> p b t q", b=2, t=4),
-        )
-        nc.vector.tensor_copy(v2s[:], tab2s[:].indirect(offs2_t[:]))
-
-        lim_t = at(LATE_VECS, "lim_t", [P, 2, 4], F32)
-        gf_t = at(LATE_VECS + 64, "gf_t", [P, 4], F32)
-        wgs_t = at(WGS, "wgs_t", [P, 4 * PS], F32)
-        load_plane(tabs, tab_scales, [nc.sync] * 4)
-        for q in (0, 2, 1, 3):
-            (nc.sync if q < 2 else nc.scalar).dma_start(wgs_t[32 * q : 32 * q + 32, :], wgs.rearrange("(q t) j -> q (t j)", t=4))
-
         def load_rows(offset, name, rows):
             raw = at(offset, name, [P, 4, rows.shape[1]], F32)
             nc.sync.dma_start(raw[:], rows.rearrange("(p j) c -> p j c", j=4))
             return raw
 
-        w1_raw = [load_rows(offset, "w1_raw%d" % a, w1[W * a : W * (a + 1), :]) for a, offset in ((0, RAW00), (1, RAW10))]
+        idx = keep.tile([P, S // 16], U16, name="idx")
+        idx2 = keep.tile([P, PS // 16], U16, name="idx2")
+        places = keep.tile([P, PS // 16], U16, name="places")
+
+        w2_plane_raw = at(SMALL + 256, "w2_plane_raw", [P, H], U8)
+        tab2_plane = at(TAB_A1 - KB, "tab2_plane", [P, TB], U8)
+        w2_raw = at(W1_A0 - KB, "w2_raw", [P, 2 * H], U8)
+        tab2 = at(W1_A1, "tab2", [P, TB], I32)
+        nc.vector.memset(tab2_plane[:].bitcast(I32), 0)
+        nc.vector.memset(w2_plane_raw[:].bitcast(I32), 0)
+        nc.sync.dma_start(idx2[:], offs2)
+        nc.sync.dma_start(places[:], pos1)
+        nc.sync.dma_start(idx[:], offs)
+        nc.sync.dma_start(w2_raw[:].bitcast(I32), w2_words[0].bitcast(I32))
+        wgs_rows = held("wgs_rows", [P, PS], F32)
+        nc.sync.dma_start(wgs_rows[:], wgs)
+        nc.sync.dma_start(tab2[:], tab2_words[0].rearrange("p t i -> p (t i)").bitcast(I32))
+        load_plane(tab2_plane, tab2_scales, [nc.sync] * 4)
+        load_plane(w2_plane_raw, w2_scales, [nc.sync] * 3 + [nc.gpsimd])
+        tab_plane = at(TAB_PLANE, "tab_plane", [P, T], U8)
+        nc.vector.memset(tab_plane[:].bitcast(I32), 0)
+
+        w2_dealt = at(W3_A1 - KB, "w2_dealt", [P, 2 * H], U8)
+        w2_plane = at(W5, "w2_plane", [P, H], U8)
+        v2 = at(STAGING + 3 * KB, "v2", [P, PS], U32)
+        v2_plane = held("v2_plane", [P, PS], U8)
+        nc.vector.tensor_copy(
+            w2_dealt[:].bitcast(U16).rearrange("p (b t q) -> p b q t", b=2, t=4),
+            w2_raw[:].bitcast(U16).rearrange("p (b q t) -> p b q t", b=2, t=4),
+        )
+        nc.vector.tensor_copy(v2[:], tab2[:].bitcast(U32).indirect(idx2[:]))
+        nc.vector.tensor_copy(v2_plane[:], tab2_plane[:].indirect(idx2[:]))
+        nc.vector.tensor_copy(
+            w2_plane[:].rearrange("p (b t q) -> p b t q", b=2, t=4),
+            w2_plane_raw[:].rearrange("p (b q t) -> p b t q", b=2, t=4),
+        )
+
+        gb_t = at(GB, "gb_t", [P, 2, 4], F32)
+        nc.gpsimd.dma_start(gb_t[:], gb.rearrange("(b p t) -> p b t", b=2, t=4))
+        lim_t = at(SMALL + KB, "lim_t", [P, 2, 4], F32)
+        gf_t = at(SMALL + KB + 64, "gf_t", [P, 4], F32)
+        wgs_t = at(WGS, "wgs_t", [P, 4 * PS], F32)
+        load_plane(tab_plane, tab_scales, [nc.sync] * 4)
+
+        identity = held("identity", [P, P], F32)
+        make_identity(nc, identity[:])
+        warm = held("warm", [P, 1], F32)
+        nc.scalar.activation(warm[:], identity[:, 0:1], ACT.Gelu_apprx_tanh)
+
+        turned = take("scan")
+        for c in range(4):
+            nc.tensor.transpose(turned[:, P * c : P * (c + 1)], wgs_rows[:, P * c : P * (c + 1)], identity[:])
+
+        def spread_wgs(t):
+            spread = held("spread%d" % t, [P, 4, 4, 32], F32)
+            picked = turned[:].rearrange("p (c q t) -> p c t q", c=4, t=4)[:, :, t, :]
+            nc.scalar.copy(spread[:], picked.unsqueeze(2).to_broadcast([P, 4, 4, 32]))
+            back = take("scan")
+            for c in range(4):
+                nc.tensor.transpose(back[:, P * c : P * (c + 1)], spread[:, c].rearrange("p r q -> p (r q)"), identity[:])
+            nc.scalar.copy(wgs_t[:, PS * t : PS * (t + 1)], back[:])
+
+        spread_wgs(0)
+
+        w1_raw = [load_rows(offset, "w1_raw%d" % a, w1[W * a : W * (a + 1), :]) for a, offset in enumerate((W1_A0, W1_A1))]
         nc.sync.dma_start(lim_t[:], lim.rearrange("(b p t) -> p b t", b=2, t=4))
         nc.sync.dma_start(gf_t[:], gf.rearrange("(p t) -> p t", t=4))
-
-        def load_words(a, offset):
-            words = at(offset, "tabw%d" % a, [P, T], I32)
+        tab = []
+        for a, offset in enumerate((TAB_A0, TAB_A1)):
+            words = at(offset, "tab%d" % a, [P, T], I32)
             nc.sync.dma_start(words[:], tab_words[a].rearrange("p t i -> p (t i)").bitcast(I32))
-            return words
+            tab.append(words)
 
-        tabw = [load_words(0, TABW0)]
-        tabw.append(load_words(1, TABW1))
-
-        vs = {}
+        halves = [idx[:, 32 * h : 32 * (h + 1)] for h in range(2)]
+        v_plane = []
         for h in range(2):
-            vs[h] = at(LATE_VECS + 128 + W * h, "vs%d" % h, [P, W], U8)
-            nc.vector.tensor_copy(vs[h][:], tabs[:].indirect(offs_t[:, 32 * h : 32 * (h + 1)]))
+            plane = at(SMALL + W * h, "v_plane%d" % h, [P, W], U8)
+            nc.vector.tensor_copy(plane[:], tab_plane[:].indirect(halves[h]))
+            v_plane.append(plane)
 
-        gated = {}
-        for u in range(8):
-            b, t = divmod(u, 4)
-            y2 = take("bank", banks)
-            nc.tensor.matmul_mx(
-                y2[:], lhsT=w2w[:, 256 * u : 256 * (u + 1)].bitcast(FP4X4), lhsT_scale=w2s[:, P * u : P * (u + 1)],
-                rhs=v2w[:].bitcast(FP8X4), rhs_scale=v2s[:], start=True, stop=True,
-            )
-            gated[u] = held("g%d" % u, [P, PS], F32)
-            nc.scalar.activation(gated[u][:], y2[:], ACT.Gelu_apprx_tanh)
-            nc.scalar.activation(gated[u][:], gated[u][:], ACT.Copy, scale=gb_t[:, b, t : t + 1])
+        scanned = {}
+        for b in range(2):
+            for t in range(4):
+                u = 4 * b + t
+                y2 = take("scan")
+                nc.tensor.matmul_mx(
+                    y2[:], lhsT=w2_dealt[:, 2 * P * u : 2 * P * (u + 1)].bitcast(FP4X4),
+                    lhsT_scale=w2_plane[:, P * u : P * (u + 1)],
+                    rhs=v2[:].bitcast(FP8X4), rhs_scale=v2_plane[:], start=True, stop=True,
+                )
+                gelu = held("gelu%d" % u, [P, PS], F32)
+                nc.scalar.activation(gelu[:], y2[:], ACT.Gelu_apprx_tanh)
+                if u == 0:
+                    scanned[b, t] = at(TAB_PLANE, "first_gained", [P, PS], F32)
+                    nc.vector.tensor_scalar(scanned[b, t][:], gelu[:], gb_t[:, b, t : t + 1], None, ALU.mult)
+                else:
+                    scanned[b, t] = gelu
+                    nc.scalar.activation(gelu[:], gelu[:], ACT.Copy, scale=gb_t[:, b, t : t + 1])
+                if b == 0 and t < 3:
+                    spread_wgs(t + 1)
 
-        w3_raw = [load_rows(offset, "w3_raw%d" % a, w3[W * a : W * (a + 1), :]) for a, offset in ((0, RAW30), (1, RAW31))]
+        w3_raw = [load_rows(offset, "w3_raw%d" % a, w3[W * a : W * (a + 1), :]) for a, offset in enumerate((W3_A0, W3_A1))]
+        w5_raw = load_rows(W5, "w5_raw", w5)
 
-        def place(u):
-            nc.vector.tensor_tensor(pages[u][:].indirect(pos_t[:]), gated[u][:], wgs_t[:, PS * (u % 4) : PS * (u % 4 + 1)], ALU.mult)
+        pages = []
 
-        for u in range(4):
-            clear(u, held("page%d" % u, [P, S], F32), nc.vector)
-            place(u)
+        def place(b, t):
+            nc.vector.tensor_tensor(pages[t][:].indirect(places[:]), scanned[b, t][:], wgs_t[:, PS * t : PS * (t + 1)], ALU.mult)
+
+        for t in range(4):
+            pages.append(held("page%d" % t, [P, S], F32))
+            nc.vector.memset(pages[t][:], 0.0)
+            place(0, t)
 
         def quantize(name, grouped, width, offset=None):
             if offset is None:
@@ -170,10 +197,10 @@ def tile_list_cylinder_wall_scores_kernel(
             return codes, scales
 
         def quantize_dealt(name, raw, offset=None):
-            grouped = take("staged", staged)
+            grouped = take("staging")
             nc.scalar.copy(
-                grouped[:].rearrange("p (t m j) -> p m j t", t=4, j=4),
-                raw.rearrange("p j (m t) -> p m j t", t=4),
+                grouped[:].rearrange("p (t q j) -> p q j t", t=4, j=4),
+                raw.rearrange("p j (q t) -> p q j t", t=4),
             )
             return quantize(name, grouped, W, offset)
 
@@ -181,155 +208,147 @@ def tile_list_cylinder_wall_scores_kernel(
         for a in range(2):
             w1_q[a, 0] = quantize_dealt("w1_%d0" % a, w1_raw[a][:, :, 0:W])
 
-        vw = {}
+        v = {}
         for h in range(2):
-            cols = offs_t[:, 32 * h : 32 * (h + 1)]
             for a in range(2):
-                vw[a, h] = held("vw%d%d" % (a, h), [P, W], U32)
-                nc.vector.tensor_copy(vw[a, h][:], tabw[a][:].bitcast(U32).indirect(cols))
+                v[a, h] = held("v%d%d" % (a, h), [P, W], U32)
+                nc.vector.tensor_copy(v[a, h][:], tab[a][:].bitcast(U32).indirect(halves[h]))
 
         for a in range(2):
-            w1_q[a, 1] = quantize_dealt("w1_%d1" % a, w1_raw[a][:, :, W : 2 * W], TABW1 + 4 * KB + 2560 * a)
+            w1_q[a, 1] = quantize_dealt("w1_%d1" % a, w1_raw[a][:, :, W : 2 * W], TAB_A1 + 4 * KB + 5 * W * a)
 
-        hist_t = [load_rows(offset, "hist%d" % h, hist[:, W * h : W * (h + 1)]) for h, offset in ((0, RAW00), (1, RAW10))]
-        w5_raw = load_rows(RAW01, "w5_raw", w5)
-        w4w = at(RAW01 + 4 * KB, "w4w", [P, 2, 2 * N], U8)
-        w4s = at(RAW01 + 5 * KB, "w4s", [P, 2 * N], U8)
-        nc.sync.dma_start(w4w[:].bitcast(I32), w4_words.rearrange("a p c -> p a c").bitcast(I32))
-        nc.gpsimd.memset(w4s[:].bitcast(I32), 0)
+        hist_t = [load_rows(offset, "hist%d" % h, hist[:, W * h : W * (h + 1)]) for h, offset in enumerate((W1_A0, W1_A1))]
+        w4 = at(W1_A0 + 12 * KB, "w4", [P, 2, 2 * N], U8)
+        w4_plane = at(W1_A0 + 13 * KB, "w4_plane", [P, 2 * N], U8)
+        nc.sync.dma_start(w4[:].bitcast(I32), w4_words.rearrange("a p c -> p a c").bitcast(I32))
+        nc.gpsimd.memset(w4_plane[:].bitcast(I32), 0)
         for q in range(4):
             nc.sync.dma_start(
-                w4s[32 * q : 32 * q + 4, :].rearrange("r (a n) -> r a n", a=2).bitcast(I32),
+                w4_plane[32 * q : 32 * q + 4, :].rearrange("r (a n) -> r a n", a=2).bitcast(I32),
                 w4_scales[:, 4 * q : 4 * q + 4, :].rearrange("a r n -> r a n").bitcast(I32),
             )
 
-        def first_stage(wq, t, h):
-            acc = take("bank", banks)
+        def first_stage(weights, t, h, acc):
             for a in range(2):
-                codes, scales = wq[a]
+                codes, scales = weights[a]
                 nc.tensor.matmul_mx(
                     acc[:], lhsT=codes[:, P * t : P * (t + 1)].bitcast(FP8X4), lhsT_scale=scales[:, P * t : P * (t + 1)],
-                    rhs=vw[a, h][:].bitcast(FP8X4), rhs_scale=vs[h][4 * a : P, :], start=(a == 0), stop=(a == 1),
+                    rhs=v[a, h][:].bitcast(FP8X4), rhs_scale=v_plane[h][4 * a : P, :], start=(a == 0), stop=(a == 1),
                 )
             return acc
 
-        def magnitudes(b, h, offsets):
-            mags = []
+        def magnitude(b, t, h, mag):
+            bank = banks[6 + h] if (b, t) == (0, 1) else take("w1")
+            acc = first_stage([w1_q[0, b], w1_q[1, b]], t, h, bank)
+            nc.scalar.activation(mag, acc[:], ACT.Abs)
+
+        def cap(b, t, z_slice, mag, cols):
+            nc.vector.scalar_tensor_tensor(z_slice, mag, lim_t[:, b, t : t + 1], pages[t][:, cols], ALU.min, ALU.add)
+
+        z_low = held("z_low", [P, 4, S], BF16)
+        z_high = [held("z_high%d" % h, [P, 4, W], BF16) for h in range(2)]
+
+        def low_slice(t, offset):
+            mag = at(offset, "mag_low%d" % t, [P, S], F32)
+            for h in range(2):
+                magnitude(0, t, h, mag[:, W * h : W * (h + 1)])
+            cap(0, t, z_low[:, t, :], mag[:], slice(0, S))
+
+        def high_magnitudes(h, offset):
+            mags = [at(offset + 2 * KB * t, "mag_high%d%d" % (h, t), [P, W], F32) for t in range(4)]
             for t in range(4):
-                acc = first_stage([w1_q[0, b], w1_q[1, b]], t, h)
-                mag = at(offsets[t], "mag%d%d%d" % (b, h, t), [P, W], F32)
-                nc.scalar.activation(mag[:], acc[:], ACT.Abs)
-                mags.append(mag)
+                magnitude(1, t, h, mags[t][:])
             return mags
 
-        def capped(b, h, mags):
-            planes = held("z%d%d" % (b, h), [P, 4, W], BF16)
+        def high_slices(h, mags):
             for t in range(4):
-                nc.vector.scalar_tensor_tensor(
-                    planes[:, t, :], mags[t][:], lim_t[:, b, t : t + 1], pages[4 * b + t][:, W * h : W * (h + 1)],
-                    ALU.min, ALU.add,
-                )
-            return planes
+                cap(1, t, z_high[h][:, t, :], mags[t][:], slice(W * h, W * (h + 1)))
 
-        def recalled(h, offsets):
-            pres = []
+        def add_hist(h, offset):
+            sums = []
             for t in range(4):
-                acc = first_stage(w3_q, t, h)
-                pre = at(offsets[t], "pre%d%d" % (h, t), [P, W], F32)
-                nc.vector.tensor_tensor(pre[:], acc[:], hist_t[h][:, t, :], ALU.add)
-                pres.append(pre)
-            return pres
+                acc = first_stage(w3_q, t, h, take("w3"))
+                total = at(offset + 2 * KB * t, "sum%d%d" % (h, t), [P, W], F32)
+                nc.vector.tensor_tensor(total[:], acc[:], hist_t[h][:, t, :], ALU.add)
+                sums.append(total)
+            return sums
 
-        def gained(h, pres, on_vector=0):
-            planes = held("f%d" % h, [P, 4, W], BF16)
+        def tanh_gain(h, sums):
+            slices = held("f%d" % h, [P, 4, W], BF16)
             for t in range(4):
-                nc.scalar.activation(pres[t][:], pres[t][:], ACT.Tanh)
-            for t in range(on_vector):
-                nc.vector.tensor_scalar(planes[:, t, :], pres[t][:], gf_t[:, t : t + 1], None, ALU.mult)
-            for t in range(on_vector, 4):
-                nc.scalar.activation(planes[:, t, :], pres[t][:], ACT.Copy, scale=gf_t[:, t : t + 1])
-            return planes
+                nc.scalar.activation(sums[t][:], sums[t][:], ACT.Tanh)
+            for t in range(4):
+                nc.scalar.activation(slices[:, t, :], sums[t][:], ACT.Copy, scale=gf_t[:, t : t + 1])
+            return slices
 
-        def woven(name, planes, shares=((0, W, nc.scalar.copy),)):
-            grouped = take("staged", staged)
-            for c0, c1, copy in shares:
-                copy(
-                    grouped[:, 4 * c0 : 4 * c1].rearrange("p (c i t) -> p c t i", i=4, t=4),
-                    planes[:, :, c0:c1].rearrange("p t (c i) -> p c t i", i=4),
-                )
+        def weave(name, slices, copy):
+            grouped = take("staging")
+            copy(
+                grouped[:].rearrange("p (c i t) -> p c t i", i=4, t=4),
+                slices.rearrange("p t (c i) -> p c t i", i=4),
+            )
             return quantize(name, grouped, W)
 
-        def second_stage(acc, n, stationary, moving, start, stop, c0=0, width=W, step=W):
-            lhsT, lhsT_scale = stationary(n)
-            codes, scales = moving
-            for c in range(0, width, step):
-                nc.tensor.matmul_mx(
-                    acc[:, c0 + c : c0 + c + step], lhsT=lhsT, lhsT_scale=lhsT_scale,
-                    rhs=codes[:, c : c + step].bitcast(FP8X4), rhs_scale=scales[:, c : c + step],
-                    start=start, stop=stop and c + step == width,
-                )
-
-        def w4_pass(b):
-            return lambda n: (w4w[:, b, 256 * n : 256 * (n + 1)].bitcast(FP4X4), w4s[:, N * b + P * n : N * b + P * (n + 1)])
-
-        def w5_pass(n):
-            return w5_q[0][:, P * n : P * (n + 1)].bitcast(FP8X4), w5_q[1][:, P * n : P * (n + 1)]
-
-        def store(scores, h, c0, width):
-            for n in range(2):
-                result = at(RAW30 + 2 * KB * (2 * h + n) + 4 * c0, "result%d%d_%d" % (n, h, c0), [P, width], F32)
-                if n == 0 or h == 0:
-                    nc.scalar.copy(result[:], scores[n][:, c0 : c0 + width])
-                else:
-                    nc.vector.tensor_copy(result[:], scores[n][:, c0 : c0 + width])
-                nc.sync.dma_start(out[P * n : P * (n + 1), W * h + c0 : W * h + c0 + width], result[:])
-
-        def quarters(*starts):
-            return [s + 2 * KB * i for s in starts for i in range(2)]
-
         def quantize_w5():
-            grouped = take("staged", staged)
+            grouped = take("staging")
             nc.vector.tensor_copy(
                 grouped[:, 0 : 4 * N].rearrange("p (c i j) -> p c j i", i=4, j=4),
                 w5_raw[:].rearrange("p j (c i) -> p c j i", i=4),
             )
             return quantize("w5", grouped, N)
 
-        mag00 = magnitudes(0, 0, quarters(TABW0, TABW0 + 4 * KB))
-        w3_q = [quantize_dealt("w3_%d" % a, w3_raw[a][:]) for a in range(2)]
-        mag01 = magnitudes(0, 1, quarters(TABW0 + 8 * KB, TABW0 + 12 * KB))
-        clear(4, at(TABW1, "page4", [P, S], F32), nc.vector)
-        place(4)
-        z00 = capped(0, 0, mag00)
-        pre0 = recalled(0, quarters(RAW30, RAW30 + 4 * KB))
-        w5_q = quantize_w5()
-        zq00 = woven("zq00", z00)
-        z01 = capped(0, 1, mag01)
-        clear(5, at(RAW00, "page5", [P, S], F32))
-        place(5)
-        f0 = gained(0, pre0)
-        pre1 = recalled(1, quarters(RAW31, RAW31 + 4 * KB))
-        fq0 = woven("fq0", f0)
-        mag10 = magnitudes(1, 0, quarters(RAW11, RAW11 + 4 * KB))
-        clear(6, at(TABW0 + 12 * KB, "page6", [P, S], F32))
-        place(6)
-        clear(7, at(RAW10, "page7", [P, S], F32))
-        place(7)
-        f1 = gained(1, pre1, 0)
-        zq01 = woven("zq01", z01)
-        mag11 = magnitudes(1, 1, quarters(TABW0, TABW0 + 4 * KB))
-        z10 = capped(1, 0, mag10)
-        z11 = capped(1, 1, mag11)
-        zq10 = woven("zq10", z10)
+        def w4_pass(b, n):
+            return w4[:, b, 2 * P * n : 2 * P * (n + 1)].bitcast(FP4X4), w4_plane[:, N * b + P * n : N * b + P * (n + 1)]
 
-        def finish(h, parts):
-            scores = [take("bank", banks) for n in range(2)]
-            for i, (stationary, moving) in enumerate(parts):
+        def w5_pass(n):
+            return w5_q[0][:, P * n : P * (n + 1)].bitcast(FP8X4), w5_q[1][:, P * n : P * (n + 1)]
+
+        def finish(h, parts, copies):
+            scores = [take("w3") for n in range(2)]
+            for i, (stationary, (codes, scales)) in enumerate(parts):
                 for n in range(2):
-                    second_stage(scores[n], n, stationary, moving, i == 0, i == 2)
-            store(scores, h, 0, W)
+                    lhsT, lhsT_scale = stationary(n)
+                    nc.tensor.matmul_mx(
+                        scores[n][:], lhsT=lhsT, lhsT_scale=lhsT_scale, rhs=codes[:].bitcast(FP8X4), rhs_scale=scales[:],
+                        start=(i == 0), stop=(i == 2),
+                    )
+            for n in range(2):
+                result = at(W3_A0 + 2 * KB * (2 * h + n), "result%d%d" % (n, h), [P, W], F32)
+                copies[n](result[:], scores[n][:])
+                nc.sync.dma_start(out[P * n : P * (n + 1), W * h : W * (h + 1)], result[:])
 
-        finish(0, ((w4_pass(0), zq00), (w5_pass, fq0), (w4_pass(1), zq10)))
-        fq1 = woven("fq1", f1)
-        zq11 = woven("zq11", z11, ((0, W, nc.vector.tensor_copy),))
-        finish(1, ((w4_pass(0), zq01), (w4_pass(1), zq11), (w5_pass, fq1)))
+        w3_q = [quantize_dealt("w3_0", w3_raw[0][:])]
+        low_slice(0, TAB_A0)
+        place(1, 0)
+        w3_q.append(quantize_dealt("w3_1", w3_raw[1][:]))
+        w5_q = quantize_w5()
+        low_slice(1, W3_A1)
+        sums0 = add_hist(0, W3_A0)
+        low_slice(2, W3_A1 + 4 * KB)
+        place(1, 1)
+        low_slice(3, TAB_A0 + 12 * KB)
+        mags0 = high_magnitudes(0, W1_A1 + 8 * KB)
+        sums1 = add_hist(1, W3_A1)
+        f0 = tanh_gain(0, sums0)
+        place(1, 2)
+        f0_q = weave("f0", f0[:], nc.scalar.copy)
+        z_low0_q = weave("z_low0", z_low[:, :, 0:W], nc.scalar.copy)
+        place(1, 3)
+        f1 = tanh_gain(1, sums1)
+        high_slices(0, mags0)
+        mags1 = high_magnitudes(1, TAB_A0)
+        z_low1_q = weave("z_low1", z_low[:, :, W:S], nc.vector.tensor_copy)
+        high_slices(1, mags1)
+        z_high0_q = weave("z_high0", z_high[0][:], nc.scalar.copy)
+        finish(
+            0,
+            ((lambda n: w4_pass(0, n), z_low0_q), (w5_pass, f0_q), (lambda n: w4_pass(1, n), z_high0_q)),
+            (nc.scalar.copy, nc.scalar.copy),
+        )
+        f1_q = weave("f1", f1[:], nc.scalar.copy)
+        z_high1_q = weave("z_high1", z_high[1][:], nc.vector.tensor_copy)
+        finish(
+            1,
+            ((lambda n: w4_pass(0, n), z_low1_q), (lambda n: w4_pass(1, n), z_high1_q), (w5_pass, f1_q)),
+            (nc.scalar.copy, nc.vector.tensor_copy),
+        )

from contextlib import ExitStack

import concourse.mybir as mybir
from concourse.masks import make_identity

K, K2, H, M, N, T, TB, S, PS = 1024, 512, 1024, 512, 256, 4096, 2048, 1024, 512
FLOPS = 2 * (K * H * S + K2 * H * PS + K * M * S + H * N * S + M * N * S)

F32 = mybir.dt.float32
BF16 = mybir.dt.bfloat16
I32 = mybir.dt.int32
U32 = mybir.dt.uint32
U16 = mybir.dt.uint16
U8 = mybir.dt.uint8
FP8X4 = mybir.dt.float8_e4m3fn_x4
FP4X4 = mybir.dt.float4_e2m1fn_x4
ALU = mybir.AluOpType
ACT = mybir.ActivationFunctionType

P = 128
W = 512
KB = 1024
STAGING_TILES = 6

WGS = 0
GB = WGS + 8 * KB
W1_A0 = GB + 64
W1_A1 = W1_A0 + 16 * KB
TAB_A0 = W1_A1 + 16 * KB
TAB_A1 = TAB_A0 + 16 * KB
SMALL = TAB_A1 + 16 * KB
W3_A0 = SMALL + 1536
W3_A1 = W3_A0 + 8 * KB
STAGING = W3_A1 + 8 * KB
W5 = STAGING + 4 * KB * STAGING_TILES
TAB_PLANE = W5 + 4 * KB


def tile_list_cylinder_wall_scores_kernel(
    tc, tab_words, tab_scales, tab2_words, tab2_scales, offs, offs2, pos1, w1, w2_words, w2_scales,
    w3, lim, gb, wgs, hist, gf, w4_words, w4_scales, w5, out,
):
    nc = tc.nc
    with ExitStack() as ctx:
        keep = ctx.enter_context(tc.tile_pool(name="keep", bufs=1))
        shared = ctx.enter_context(tc.tile_pool(name="shared", bufs=1))
        psum = ctx.enter_context(tc.psum_pool(name="psum", bufs=1))

        def held(name, shape, dtype):
            return keep.tile(shape, dtype, name=name, align_bytes=64)

        def at(offset, name, shape, dtype):
            return shared.tile(shape, dtype, name=name, align_bytes=64, offset=offset)

        banks = [psum.tile([P, W], F32, name="bank%d" % i) for i in range(8)]
        staging = [at(STAGING + 4 * KB * i, "staging%d" % i, [P, 4 * W], BF16) for i in range(STAGING_TILES)]
        rings = {"scan": banks, "w1": banks[0:4], "w3": banks[4:8], "staging": staging}
        turns = {ring: 0 for ring in rings}

        def take(ring):
            tile = rings[ring][turns[ring] % len(rings[ring])]
            turns[ring] = turns[ring] + 1
            return tile

        def load_plane(plane, scales, queues):
            rows = 4 * scales.shape[0]
            for q in range(4):
                queues[q].dma_start(plane[32 * q : 32 * q + rows, :].bitcast(I32), scales[:, 4 * q : 4 * q + 4, :].bitcast(I32))

        def load_rows(offset, name, rows):
            raw = at(offset, name, [P, 4, rows.shape[1]], F32)
            nc.sync.dma_start(raw[:], rows.rearrange("(p j) c -> p j c", j=4))
            return raw

        idx = keep.tile([P, S // 16], U16, name="idx")
        idx2 = keep.tile([P, PS // 16], U16, name="idx2")
        places = keep.tile([P, PS // 16], U16, name="places")

        w2_plane_raw = at(SMALL + 256, "w2_plane_raw", [P, H], U8)
        tab2_plane = at(TAB_A1 - KB, "tab2_plane", [P, TB], U8)
        w2_raw = at(W1_A0 - KB, "w2_raw", [P, 2 * H], U8)
        tab2 = at(W1_A1, "tab2", [P, TB], I32)
        nc.vector.memset(tab2_plane[:].bitcast(I32), 0)
        nc.vector.memset(w2_plane_raw[:].bitcast(I32), 0)
        nc.sync.dma_start(idx2[:], offs2)
        nc.sync.dma_start(places[:], pos1)
        nc.sync.dma_start(idx[:], offs)
        nc.sync.dma_start(w2_raw[:].bitcast(I32), w2_words[0].bitcast(I32))
        wgs_rows = held("wgs_rows", [P, PS], F32)
        nc.sync.dma_start(wgs_rows[:], wgs)
        nc.sync.dma_start(tab2[:], tab2_words[0].rearrange("p t i -> p (t i)").bitcast(I32))
        load_plane(tab2_plane, tab2_scales, [nc.sync] * 4)
        load_plane(w2_plane_raw, w2_scales, [nc.sync] * 3 + [nc.gpsimd])
        tab_plane = at(TAB_PLANE, "tab_plane", [P, T], U8)
        nc.vector.memset(tab_plane[:].bitcast(I32), 0)

        w2_dealt = at(W3_A1 - KB, "w2_dealt", [P, 2 * H], U8)
        w2_plane = at(W5, "w2_plane", [P, H], U8)
        v2 = at(STAGING + 3 * KB, "v2", [P, PS], U32)
        v2_plane = held("v2_plane", [P, PS], U8)
        nc.vector.tensor_copy(
            w2_dealt[:].bitcast(U16).rearrange("p (b t q) -> p b q t", b=2, t=4),
            w2_raw[:].bitcast(U16).rearrange("p (b q t) -> p b q t", b=2, t=4),
        )
        nc.vector.tensor_copy(v2[:], tab2[:].bitcast(U32).indirect(idx2[:]))
        nc.vector.tensor_copy(v2_plane[:], tab2_plane[:].indirect(idx2[:]))
        nc.vector.tensor_copy(
            w2_plane[:].rearrange("p (b t q) -> p b t q", b=2, t=4),
            w2_plane_raw[:].rearrange("p (b q t) -> p b t q", b=2, t=4),
        )

        gb_t = at(GB, "gb_t", [P, 2, 4], F32)
        nc.gpsimd.dma_start(gb_t[:], gb.rearrange("(b p t) -> p b t", b=2, t=4))
        lim_t = at(SMALL + KB, "lim_t", [P, 2, 4], F32)
        gf_t = at(SMALL + KB + 64, "gf_t", [P, 4], F32)
        wgs_t = at(WGS, "wgs_t", [P, 4 * PS], F32)
        load_plane(tab_plane, tab_scales, [nc.sync] * 4)

        identity = held("identity", [P, P], F32)
        make_identity(nc, identity[:])
        warm = held("warm", [P, 1], F32)
        nc.scalar.activation(warm[:], identity[:, 0:1], ACT.Gelu_apprx_tanh)

        turned = take("scan")
        for c in range(4):
            nc.tensor.transpose(turned[:, P * c : P * (c + 1)], wgs_rows[:, P * c : P * (c + 1)], identity[:])

        def spread_wgs(t):
            spread = held("spread%d" % t, [P, 4, 4, 32], F32)
            picked = turned[:].rearrange("p (c q t) -> p c t q", c=4, t=4)[:, :, t, :]
            nc.scalar.copy(spread[:], picked.unsqueeze(2).to_broadcast([P, 4, 4, 32]))
            back = take("scan")
            for c in range(4):
                nc.tensor.transpose(back[:, P * c : P * (c + 1)], spread[:, c].rearrange("p r q -> p (r q)"), identity[:])
            nc.scalar.copy(wgs_t[:, PS * t : PS * (t + 1)], back[:])

        spread_wgs(0)

        w1_raw = [load_rows(offset, "w1_raw%d" % a, w1[W * a : W * (a + 1), :]) for a, offset in enumerate((W1_A0, W1_A1))]
        nc.sync.dma_start(lim_t[:], lim.rearrange("(b p t) -> p b t", b=2, t=4))
        nc.sync.dma_start(gf_t[:], gf.rearrange("(p t) -> p t", t=4))
        tab = []
        for a, offset in enumerate((TAB_A0, TAB_A1)):
            words = at(offset, "tab%d" % a, [P, T], I32)
            nc.sync.dma_start(words[:], tab_words[a].rearrange("p t i -> p (t i)").bitcast(I32))
            tab.append(words)

        halves = [idx[:, 32 * h : 32 * (h + 1)] for h in range(2)]
        v_plane = []
        for h in range(2):
            plane = at(SMALL + W * h, "v_plane%d" % h, [P, W], U8)
            nc.vector.tensor_copy(plane[:], tab_plane[:].indirect(halves[h]))
            v_plane.append(plane)

        scanned = {}
        for b in range(2):
            for t in range(4):
                u = 4 * b + t
                y2 = take("scan")
                nc.tensor.matmul_mx(
                    y2[:], lhsT=w2_dealt[:, 2 * P * u : 2 * P * (u + 1)].bitcast(FP4X4),
                    lhsT_scale=w2_plane[:, P * u : P * (u + 1)],
                    rhs=v2[:].bitcast(FP8X4), rhs_scale=v2_plane[:], start=True, stop=True,
                )
                gelu = held("gelu%d" % u, [P, PS], F32)
                nc.scalar.activation(gelu[:], y2[:], ACT.Gelu_apprx_tanh)
                if u == 0:
                    scanned[b, t] = at(TAB_PLANE, "first_gained", [P, PS], F32)
                    nc.vector.tensor_scalar(scanned[b, t][:], gelu[:], gb_t[:, b, t : t + 1], None, ALU.mult)
                else:
                    scanned[b, t] = gelu
                    nc.scalar.activation(gelu[:], gelu[:], ACT.Copy, scale=gb_t[:, b, t : t + 1])
                if b == 0 and t < 3:
                    spread_wgs(t + 1)

        w3_raw = [load_rows(offset, "w3_raw%d" % a, w3[W * a : W * (a + 1), :]) for a, offset in enumerate((W3_A0, W3_A1))]
        w5_raw = load_rows(W5, "w5_raw", w5)

        pages = []

        def place(b, t):
            nc.vector.tensor_tensor(pages[t][:].indirect(places[:]), scanned[b, t][:], wgs_t[:, PS * t : PS * (t + 1)], ALU.mult)

        for t in range(4):
            pages.append(held("page%d" % t, [P, S], F32))
            nc.vector.memset(pages[t][:], 0.0)
            place(0, t)

        def quantize(name, grouped, width, offset=None):
            if offset is None:
                codes = held(name + "_codes", [P, width], U32)
                scales = held(name + "_scales", [P, width], U8)
            else:
                codes = at(offset, name + "_codes", [P, width], U32)
                scales = at(offset + 4 * width, name + "_scales", [P, width], U8)
            nc.vector.quantize_mx(codes[:].bitcast(FP8X4), scales[:], grouped[:, 0 : 4 * width])
            return codes, scales

        def quantize_dealt(name, raw, offset=None):
            grouped = take("staging")
            nc.scalar.copy(
                grouped[:].rearrange("p (t q j) -> p q j t", t=4, j=4),
                raw.rearrange("p j (q t) -> p q j t", t=4),
            )
            return quantize(name, grouped, W, offset)

        w1_q = {}
        for a in range(2):
            w1_q[a, 0] = quantize_dealt("w1_%d0" % a, w1_raw[a][:, :, 0:W])

        v = {}
        for h in range(2):
            for a in range(2):
                v[a, h] = held("v%d%d" % (a, h), [P, W], U32)
                nc.vector.tensor_copy(v[a, h][:], tab[a][:].bitcast(U32).indirect(halves[h]))

        for a in range(2):
            w1_q[a, 1] = quantize_dealt("w1_%d1" % a, w1_raw[a][:, :, W : 2 * W], TAB_A1 + 4 * KB + 5 * W * a)

        hist_t = [load_rows(offset, "hist%d" % h, hist[:, W * h : W * (h + 1)]) for h, offset in enumerate((W1_A0, W1_A1))]
        w4 = at(W1_A0 + 12 * KB, "w4", [P, 2, 2 * N], U8)
        w4_plane = at(W1_A0 + 13 * KB, "w4_plane", [P, 2 * N], U8)
        nc.sync.dma_start(w4[:].bitcast(I32), w4_words.rearrange("a p c -> p a c").bitcast(I32))
        nc.gpsimd.memset(w4_plane[:].bitcast(I32), 0)
        for q in range(4):
            nc.sync.dma_start(
                w4_plane[32 * q : 32 * q + 4, :].rearrange("r (a n) -> r a n", a=2).bitcast(I32),
                w4_scales[:, 4 * q : 4 * q + 4, :].rearrange("a r n -> r a n").bitcast(I32),
            )

        def first_stage(weights, t, h, acc):
            for a in range(2):
                codes, scales = weights[a]
                nc.tensor.matmul_mx(
                    acc[:], lhsT=codes[:, P * t : P * (t + 1)].bitcast(FP8X4), lhsT_scale=scales[:, P * t : P * (t + 1)],
                    rhs=v[a, h][:].bitcast(FP8X4), rhs_scale=v_plane[h][4 * a : P, :], start=(a == 0), stop=(a == 1),
                )
            return acc

        def magnitude(b, t, h, mag):
            bank = banks[6 + h] if (b, t) == (0, 1) else take("w1")
            acc = first_stage([w1_q[0, b], w1_q[1, b]], t, h, bank)
            nc.scalar.activation(mag, acc[:], ACT.Abs)

        def cap(b, t, z_slice, mag, cols):
            nc.vector.scalar_tensor_tensor(z_slice, mag, lim_t[:, b, t : t + 1], pages[t][:, cols], ALU.min, ALU.add)

        z_low = held("z_low", [P, 4, S], BF16)
        z_high = [held("z_high%d" % h, [P, 4, W], BF16) for h in range(2)]

        def low_slice(t, offset):
            mag = at(offset, "mag_low%d" % t, [P, S], F32)
            for h in range(2):
                magnitude(0, t, h, mag[:, W * h : W * (h + 1)])
            cap(0, t, z_low[:, t, :], mag[:], slice(0, S))

        def high_magnitudes(h, offset):
            mags = [at(offset + 2 * KB * t, "mag_high%d%d" % (h, t), [P, W], F32) for t in range(4)]
            for t in range(4):
                magnitude(1, t, h, mags[t][:])
            return mags

        def high_slices(h, mags):
            for t in range(4):
                cap(1, t, z_high[h][:, t, :], mags[t][:], slice(W * h, W * (h + 1)))

        def add_hist(h, offset):
            sums = []
            for t in range(4):
                acc = first_stage(w3_q, t, h, take("w3"))
                total = at(offset + 2 * KB * t, "sum%d%d" % (h, t), [P, W], F32)
                nc.vector.tensor_tensor(total[:], acc[:], hist_t[h][:, t, :], ALU.add)
                sums.append(total)
            return sums

        def tanh_gain(h, sums):
            slices = held("f%d" % h, [P, 4, W], BF16)
            for t in range(4):
                nc.scalar.activation(sums[t][:], sums[t][:], ACT.Tanh)
            for t in range(4):
                nc.scalar.activation(slices[:, t, :], sums[t][:], ACT.Copy, scale=gf_t[:, t : t + 1])
            return slices

        def weave(name, slices, copy):
            grouped = take("staging")
            copy(
                grouped[:].rearrange("p (c i t) -> p c t i", i=4, t=4),
                slices.rearrange("p t (c i) -> p c t i", i=4),
            )
            return quantize(name, grouped, W)

        def quantize_w5():
            grouped = take("staging")
            nc.vector.tensor_copy(
                grouped[:, 0 : 4 * N].rearrange("p (c i j) -> p c j i", i=4, j=4),
                w5_raw[:].rearrange("p j (c i) -> p c j i", i=4),
            )
            return quantize("w5", grouped, N)

        def w4_pass(b, n):
            return w4[:, b, 2 * P * n : 2 * P * (n + 1)].bitcast(FP4X4), w4_plane[:, N * b + P * n : N * b + P * (n + 1)]

        def w5_pass(n):
            return w5_q[0][:, P * n : P * (n + 1)].bitcast(FP8X4), w5_q[1][:, P * n : P * (n + 1)]

        def finish(h, parts, copies):
            scores = [take("w3") for n in range(2)]
            for i, (stationary, (codes, scales)) in enumerate(parts):
                for n in range(2):
                    lhsT, lhsT_scale = stationary(n)
                    nc.tensor.matmul_mx(
                        scores[n][:], lhsT=lhsT, lhsT_scale=lhsT_scale, rhs=codes[:].bitcast(FP8X4), rhs_scale=scales[:],
                        start=(i == 0), stop=(i == 2),
                    )
            for n in range(2):
                result = at(W3_A0 + 2 * KB * (2 * h + n), "result%d%d" % (n, h), [P, W], F32)
                copies[n](result[:], scores[n][:])
                nc.sync.dma_start(out[P * n : P * (n + 1), W * h : W * (h + 1)], result[:])

        w3_q = [quantize_dealt("w3_0", w3_raw[0][:])]
        low_slice(0, TAB_A0)
        place(1, 0)
        w3_q.append(quantize_dealt("w3_1", w3_raw[1][:]))
        w5_q = quantize_w5()
        low_slice(1, W3_A1)
        sums0 = add_hist(0, W3_A0)
        low_slice(2, W3_A1 + 4 * KB)
        place(1, 1)
        low_slice(3, TAB_A0 + 12 * KB)
        mags0 = high_magnitudes(0, W1_A1 + 8 * KB)
        sums1 = add_hist(1, W3_A1)
        f0 = tanh_gain(0, sums0)
        place(1, 2)
        f0_q = weave("f0", f0[:], nc.scalar.copy)
        z_low0_q = weave("z_low0", z_low[:, :, 0:W], nc.scalar.copy)
        place(1, 3)
        f1 = tanh_gain(1, sums1)
        high_slices(0, mags0)
        mags1 = high_magnitudes(1, TAB_A0)
        z_low1_q = weave("z_low1", z_low[:, :, W:S], nc.vector.tensor_copy)
        high_slices(1, mags1)
        z_high0_q = weave("z_high0", z_high[0][:], nc.scalar.copy)
        finish(
            0,
            ((lambda n: w4_pass(0, n), z_low0_q), (w5_pass, f0_q), (lambda n: w4_pass(1, n), z_high0_q)),
            (nc.scalar.copy, nc.scalar.copy),
        )
        f1_q = weave("f1", f1[:], nc.scalar.copy)
        z_high1_q = weave("z_high1", z_high[1][:], nc.vector.tensor_copy)
        finish(
            1,
            ((lambda n: w4_pass(0, n), z_low1_q), (lambda n: w4_pass(1, n), z_high1_q), (w5_pass, f1_q)),
            (nc.scalar.copy, nc.vector.tensor_copy),
        )
